import numpy as np
import ml_dtypes


def mxq(x, axis, fmt="e4m3"):
    dtype, down = {"e4m3": (ml_dtypes.float8_e4m3fn, 7), "e5m2": (ml_dtypes.float8_e5m2, 14)}[fmt]
    v = np.moveaxis(np.asarray(x, np.float32).astype(ml_dtypes.bfloat16).astype(np.float64), axis, -1)
    blocks = v.reshape(v.shape[:-1] + (-1, 32))
    amax = np.abs(blocks).max(-1, keepdims=True)
    byte = np.maximum(np.where(amax > 0, np.frexp(amax)[1] - 1 + 127, 0) - down, 1)
    scale = np.exp2(byte - 127.0)
    codes = (blocks / scale).astype(np.float32).astype(dtype).astype(np.float64)
    return np.moveaxis((codes * scale).reshape(v.shape), -1, axis)


WIDE = False


def mx_kscale(k):
    if not WIDE:
        return np.ones(k)
    levels = np.array([10, -10, 5, -5, 0])
    if k % 512:
        return np.exp2(np.random.permutation(np.resize(levels, k // 32))).repeat(32)
    a = np.empty((k // 512, 16))
    for p in range(k // 512):
        a[p, :8] = np.random.permutation(np.resize(levels, 8))
        for g in range(8):
            far = levels[np.abs(levels - a[p, g]) >= 10]
            a[p, g + 8] = far[np.random.randint(len(far))]
    return np.exp2(a.ravel()).repeat(32)


def f64(x):
    return np.asarray(x).astype(np.float64)


def striped8(idx):
    return np.concatenate([v.reshape(-1, 16).T for v in idx]).astype(np.uint16)


def unstriped8(offs):
    return np.stack([offs[16 * g:16 * g + 16].T.reshape(-1) for g in range(8)]).astype(np.int64)


def split(x):
    m, e = np.frexp(f64(x))
    hi = np.ldexp(np.trunc(16.0 * m) / 16.0, e)
    return hi, f64(x) - hi


K, M, T, S = 1024, 512, 2048, 1024


def setup_inputs():
    n = np.random.standard_normal
    s = mx_kscale(K)[:, None]
    return {
        "xT": (n((K, T)) * s).astype(np.float32),
        "w": (n((K, M)) / np.sqrt(K) / s).astype(np.float32),
        "wgt": np.repeat(np.random.uniform(0.5, 2.0, (8, S)), 16, axis=0).astype(np.float32),
        "b": (0.3 * n(512)).astype(np.float32),
        "offs": striped8(np.stack([np.random.permutation(T)[:S] for _ in range(8)])),
    }


def reference(xT, w, wgt, b, offs):
    idx = unstriped8(offs)
    group = np.arange(K) % 512 // 64
    xg = f64(wgt)[np.arange(K) // 4 % 128] * f64(xT)[np.arange(K)[:, None], idx[group]]
    xT_ = mxq(xg, 0, "e4m3")
    w_hi, w_lo = split(w)
    w_hi_, w_lo_ = mxq(w_hi, 0, "e4m3"), mxq(w_lo, 0, "e4m3")
    y = xT_.T @ w_hi_ + xT_.T @ w_lo_
    return y + f64(b)[None, :]

@@ -1,0 +1,207 @@
+import concourse.mybir as mybir
+
+K, M, T, S = 1024, 512, 2048, 1024
+P = 128
+PACK = 4
+PASSES = K // (P * PACK)
+
+F32 = mybir.dt.float32
+BF16 = mybir.dt.bfloat16
+I32 = mybir.dt.int32
+U32 = mybir.dt.uint32
+U16 = mybir.dt.uint16
+U8 = mybir.dt.uint8
+FP8X4 = mybir.dt.float8_e4m3fn_x4
+ALU = mybir.AluOpType
+
+FLOPS = 2 * 2 * K * M * S
+FIRST = 640
+PLANE_ORDER = ((0, 0), (0, 1), (0, 2), (1, 0), (1, 1), (0, 3), (1, 2), (1, 3))
+HI_MASK = -0x000F0010
+
+
+def tile_list_heads_tm_hl_bias_kernel(tc, xT, w, wgt, b, offs, out):
+    nc = tc.nc
+    x_view = xT.rearrange("(a p i) t -> a i p t", a=PASSES, i=PACK)
+    w_view = w.rearrange("(a p i) n -> a p i n", a=PASSES, i=PACK)
+
+    with (
+        tc.tile_pool(name="lists", bufs=1) as lists,
+        tc.tile_pool(name="keep", bufs=1) as keep,
+        tc.psum_pool(name="psum", bufs=1) as psum,
+    ):
+        offsets = lists.tile([P, S // 16], U16, name="offsets")
+        wgt_sb = keep.tile([P, S], F32, name="wgt_sb")
+        wgt_late = keep.tile([P, S - FIRST], F32, name="wgt_late")
+        bias = keep.tile([P, M], F32, name="bias")
+        planes = [[keep.tile([P, T], F32, name=f"plane{a}{i}") for i in range(PACK)] for a in range(PASSES)]
+        w_sb = [keep.tile([P, PACK, M], F32, name=f"w_sb{a}") for a in range(PASSES)]
+        w_raw = keep.tile([P, M, PACK], BF16, name="w_raw", align_bytes=64)
+        parts = [keep.tile([P, 2, M, PACK], BF16, name=f"parts{a}", align_bytes=64) for a in range(PASSES)]
+        w_codes = [keep.tile([P, 2 * M], U32, name=f"w_codes{a}", align_bytes=64) for a in range(PASSES)]
+        w_scales = [keep.tile([P, 2 * M], U8, name=f"w_scales{a}", align_bytes=64) for a in range(PASSES)]
+        hi32 = keep.tile([P, PACK, M], F32, name="hi32")
+        picked = [keep.tile([P, PACK, S], F32, name=f"picked{a}") for a in range(PASSES)]
+        x_bf = [keep.tile([P, S, PACK], BF16, name=f"x_bf{a}", align_bytes=64) for a in range(PASSES)]
+        x_codes = [keep.tile([P, S], U32, name=f"x_codes{a}", align_bytes=64) for a in range(PASSES)]
+        x_scales = [keep.tile([P, S], U8, name=f"x_scales{a}", align_bytes=64) for a in range(PASSES)]
+        acc = [psum.tile([P, M], F32, name=f"acc{j}") for j in range(S // P)]
+        result = [keep.tile([P, M], F32, name=f"result{j}") for j in range(S // P)]
+
+        def load_w(a, i0, i1):
+            nc.sync.dma_start(out=w_sb[a][:, i0:i1, :], in_=w_view[a][:, i0:i1, :])
+
+        def load_plane(a, i):
+            nc.sync.dma_start(out=planes[a][i][:], in_=x_view[a, i])
+
+        def raw_w(n0, n1):
+            upper = w_sb[1][:].bitcast(BF16).rearrange("p i (n h) -> p i n h", h=2)[:, :, n0:n1, 1]
+            nc.scalar.copy(
+                out=w_raw[:, n0:n1, :].rearrange("p (c e) i -> p c i e", e=4),
+                in_=upper.rearrange("p i (c e) -> p c i e", e=4),
+            )
+
+        def mask_packed(n0, n1):
+            nc.vector.tensor_scalar(
+                out=parts[1][:, 0, n0:n1, :].rearrange("p n i -> p (n i)").bitcast(I32),
+                in0=w_raw[:, n0:n1, :].rearrange("p n i -> p (n i)").bitcast(I32),
+                scalar1=HI_MASK,
+                scalar2=None,
+                op0=ALU.bitwise_and,
+            )
+
+        def mask_rows(i0, i1):
+            nc.vector.tensor_scalar(
+                out=hi32[:, i0:i1, :].bitcast(I32),
+                in0=w_sb[0][:, i0:i1, :].bitcast(I32),
+                scalar1=-0x00100000,
+                scalar2=None,
+                op0=ALU.bitwise_and,
+            )
+
+        def cast_hi():
+            nc.scalar.copy(
+                out=parts[0][:, 0, :, :].rearrange("p (c e) i -> p c i e", e=4),
+                in_=hi32[:].rearrange("p i (c e) -> p c i e", e=4),
+            )
+
+        def rest_w(a, n0, n1):
+            if a == 0:
+                hi = hi32[:, :, n0:n1].rearrange("p i (c e) -> p c i e", e=4)
+            else:
+                hi = parts[a][:, 0, n0:n1, :].rearrange("p (c e) i -> p c i e", e=4)
+            nc.vector.tensor_tensor(
+                out=parts[a][:, 1, n0:n1, :].rearrange("p (c e) i -> p c i e", e=4),
+                in0=w_sb[a][:, :, n0:n1].rearrange("p i (c e) -> p c i e", e=4),
+                in1=hi,
+                op=ALU.subtract,
+            )
+
+        def quantize_w(a, h):
+            nc.vector.quantize_mx(
+                out=w_codes[a][:, h * M : (h + 1) * M].bitcast(FP8X4),
+                scales=w_scales[a][:, h * M : (h + 1) * M],
+                in_=parts[a][:, h, :, :].rearrange("p n i -> p (n i)"),
+            )
+
+        def gather(a, i, j0, c):
+            late = a == 1 and j0 >= FIRST
+            weights = wgt_late[:, j0 - FIRST : j0 - FIRST + c] if late else wgt_sb[:, j0 : j0 + c]
+            nc.vector.tensor_tensor(
+                out=picked[a][:, i, j0 : j0 + c],
+                in0=planes[a][i][:].indirect(offsets[:, j0 // 16 : (j0 + c) // 16]),
+                in1=weights,
+                op=ALU.mult,
+            )
+
+        def interleave_x(a, j0, c):
+            nc.scalar.copy(
+                out=x_bf[a][:, j0 : j0 + c, :].rearrange("p (c e) i -> p c i e", e=4),
+                in_=picked[a][:, :, j0 : j0 + c].rearrange("p i (c e) -> p c i e", e=4),
+            )
+
+        def quantize_x(a, j0, c):
+            nc.vector.quantize_mx(
+                out=x_codes[a][:, j0 : j0 + c].bitcast(FP8X4),
+                scales=x_scales[a][:, j0 : j0 + c],
+                in_=x_bf[a][:, j0 : j0 + c, :].rearrange("p j i -> p (j i)"),
+            )
+
+        def multiply(a, j0, c):
+            for j in range(j0 // P, (j0 + c) // P):
+                cols = slice(j * P, (j + 1) * P)
+                for k in range(2):
+                    w_cols = slice(k * M, (k + 1) * M)
+                    nc.tensor.matmul_mx(
+                        out=acc[j][:],
+                        lhsT=x_codes[a][:, cols].bitcast(FP8X4),
+                        lhsT_scale=x_scales[a][:, cols],
+                        rhs=w_codes[a][:, w_cols].bitcast(FP8X4),
+                        rhs_scale=w_scales[a][:, w_cols],
+                        start=(a == 0 and k == 0),
+                        stop=(a == PASSES - 1 and k == 1),
+                    )
+
+        def finish(j0, c):
+            for j in range(j0 // P, (j0 + c) // P):
+                nc.vector.tensor_tensor(out=result[j][:], in0=acc[j][:], in1=bias[:], op=ALU.add)
+                nc.sync.dma_start(out=out[j * P : (j + 1) * P, :], in_=result[j][:])
+
+        load_w(0, 0, 2)
+        load_w(0, 2, 4)
+        load_w(1, 0, 4)
+        nc.sync.dma_start(offsets[:], offs)
+        nc.sync.dma_start(out=wgt_sb[:], in_=wgt)
+        for a, i in PLANE_ORDER:
+            load_plane(a, i)
+        nc.sync.dma_start(out=wgt_late[:], in_=wgt[:, FIRST:S])
+        nc.sync.dma_start(out=bias[:], in_=b.partition_broadcast(P))
+
+        mask_rows(0, 2)
+        mask_rows(2, 4)
+        rest_w(0, 0, 256)
+        rest_w(0, 256, 512)
+        cast_hi()
+        raw_w(0, 256)
+        raw_w(256, 512)
+        mask_packed(0, 256)
+        quantize_w(0, 1)
+        rest_w(1, 0, 256)
+        mask_packed(256, 512)
+        quantize_w(0, 0)
+        rest_w(1, 256, 512)
+        quantize_w(1, 0)
+        gather(0, 0, 0, 512)
+        quantize_w(1, 1)
+        gather(0, 0, 512, 512)
+        for i in (1, 2):
+            gather(0, i, 0, 512)
+            gather(0, i, 512, 512)
+        gather(1, 0, 0, 640)
+        gather(1, 1, 0, 640)
+        gather(0, 3, 0, 512)
+        interleave_x(0, 0, 256)
+        interleave_x(0, 256, 256)
+        gather(0, 3, 512, 512)
+        interleave_x(0, 512, 256)
+        interleave_x(0, 768, 256)
+        gather(1, 2, 0, 640)
+        quantize_x(0, 0, 256)
+        multiply(0, 0, 256)
+        gather(1, 3, 0, 640)
+        for j0 in (256, 512, 768):
+            quantize_x(0, j0, 256)
+            multiply(0, j0, 256)
+        for j0, c in ((0, 256), (256, 256), (512, 128)):
+            interleave_x(1, j0, c)
+        for i in range(3):
+            gather(1, i, 640, 384)
+        quantize_x(1, 0, 256)
+        multiply(1, 0, 256)
+        gather(1, 3, 640, 384)
+        interleave_x(1, 640, 256)
+        interleave_x(1, 896, 128)
+        for j0, c in ((256, 256), (512, 128), (640, 256), (896, 128)):
+            quantize_x(1, j0, c)
+            multiply(1, j0, c)
+        finish(0, 1024)

@@ -1,4 +1,5 @@
 import concourse.mybir as mybir
+from concourse.masks import make_identity
 
 K, M, T, S = 1024, 512, 2048, 1024
 P = 128
@@ -13,11 +14,13 @@ U16 = mybir.dt.uint16
 U8 = mybir.dt.uint8
 FP8X4 = mybir.dt.float8_e4m3fn_x4
 ALU = mybir.AluOpType
+ACT = mybir.ActivationFunctionType
 
 FLOPS = 2 * 2 * K * M * S
-FIRST = 640
+PIECE = 256
 PLANE_ORDER = ((0, 0), (0, 1), (0, 2), (1, 0), (1, 1), (0, 3), (1, 2), (1, 3))
-HI_MASK = -0x000F0010
+HI_MASK = -0x00100000
+SIGN_BIT = -0x80000000
 
 
 def tile_list_heads_tm_hl_bias_kernel(tc, xT, w, wgt, b, offs, out):
@@ -32,15 +35,17 @@ def tile_list_heads_tm_hl_bias_kernel(tc, xT, w, wgt, b, offs, out):
     ):
         offsets = lists.tile([P, S // 16], U16, name="offsets")
         wgt_sb = keep.tile([P, S], F32, name="wgt_sb")
-        wgt_late = keep.tile([P, S - FIRST], F32, name="wgt_late")
         bias = keep.tile([P, M], F32, name="bias")
         planes = [[keep.tile([P, T], F32, name=f"plane{a}{i}") for i in range(PACK)] for a in range(PASSES)]
-        w_sb = [keep.tile([P, PACK, M], F32, name=f"w_sb{a}") for a in range(PASSES)]
-        w_raw = keep.tile([P, M, PACK], BF16, name="w_raw", align_bytes=64)
+        w_first = [keep.tile([P, PACK, M // 2], F32, name=f"w_first{h}") for h in range(2)]
+        w_second = keep.tile([P, PACK, M], F32, name="w_second")
+        ident = keep.tile([P, P], F32, name="ident")
+        neg_hi = keep.tile([P, PACK, M], F32, name="neg_hi")
+        lo_turned = keep.tile([P, M // P, 2, P, 2], BF16, name="lo_turned", align_bytes=64)
         parts = [keep.tile([P, 2, M, PACK], BF16, name=f"parts{a}", align_bytes=64) for a in range(PASSES)]
         w_codes = [keep.tile([P, 2 * M], U32, name=f"w_codes{a}", align_bytes=64) for a in range(PASSES)]
         w_scales = [keep.tile([P, 2 * M], U8, name=f"w_scales{a}", align_bytes=64) for a in range(PASSES)]
-        hi32 = keep.tile([P, PACK, M], F32, name="hi32")
+        hi32 = [keep.tile([P, PACK, M // 2], F32, name=f"hi32{h}") for h in range(2)]
         picked = [keep.tile([P, PACK, S], F32, name=f"picked{a}") for a in range(PASSES)]
         x_bf = [keep.tile([P, S, PACK], BF16, name=f"x_bf{a}", align_bytes=64) for a in range(PASSES)]
         x_codes = [keep.tile([P, S], U32, name=f"x_codes{a}", align_bytes=64) for a in range(PASSES)]
@@ -48,69 +53,90 @@ def tile_list_heads_tm_hl_bias_kernel(tc, xT, w, wgt, b, offs, out):
         acc = [psum.tile([P, M], F32, name=f"acc{j}") for j in range(S // P)]
         result = [keep.tile([P, M], F32, name=f"result{j}") for j in range(S // P)]
 
-        def load_w(a, i0, i1):
-            nc.sync.dma_start(out=w_sb[a][:, i0:i1, :], in_=w_view[a][:, i0:i1, :])
-
         def load_plane(a, i):
             nc.sync.dma_start(out=planes[a][i][:], in_=x_view[a, i])
 
-        def raw_w(n0, n1):
-            upper = w_sb[1][:].bitcast(BF16).rearrange("p i (n h) -> p i n h", h=2)[:, :, n0:n1, 1]
-            nc.scalar.copy(
-                out=w_raw[:, n0:n1, :].rearrange("p (c e) i -> p c i e", e=4),
-                in_=upper.rearrange("p i (c e) -> p c i e", e=4),
+        def mask_negated():
+            nc.vector.tensor_scalar(
+                out=neg_hi[:].bitcast(I32),
+                in0=w_second[:].bitcast(I32),
+                scalar1=HI_MASK,
+                scalar2=SIGN_BIT,
+                op0=ALU.bitwise_and,
+                op1=ALU.bitwise_xor,
             )
 
-        def mask_packed(n0, n1):
+        def cast_negated(n0, n1):
+            nc.scalar.activation(
+                out=parts[1][:, 0, n0:n1, :].rearrange("p (c e) i -> p c i e", e=4),
+                in_=neg_hi[:, :, n0:n1].rearrange("p i (c e) -> p c i e", e=4),
+                func=ACT.Copy,
+                scale=-1.0,
+            )
+
+        def turn_rest(nb):
+            bank = acc[nb]
+            cols = slice(nb * P, (nb + 1) * P)
+            for i in range(PACK):
+                target = bank[:, i * P : (i + 1) * P]
+                nc.tensor.matmul(target, lhsT=w_second[:, i, cols], rhs=ident[:], start=True, stop=False, is_transpose=True)
+                nc.tensor.matmul(target, lhsT=neg_hi[:, i, cols], rhs=ident[:], start=False, stop=True, is_transpose=True)
+            nc.scalar.copy(
+                out=lo_turned[:, nb, :, :, :],
+                in_=bank[:].rearrange("n (u e p) -> n u p e", u=2, e=2),
+            )
+
+        def turn_back(h):
+            bank = acc[4 + h]
+            words = lo_turned[:].rearrange("n b u p e -> n (b u p e)").bitcast(F32)
+            for u in range(2):
+                for b2 in range(2):
+                    at = ((2 * h + b2) * 2 + u) * P
+                    to = (2 * u + b2) * P
+                    nc.tensor.transpose(bank[:, to : to + P], words[:, at : at + P], ident[:])
+            nc.scalar.copy(
+                out=parts[1][:, 1, h * 256 : (h + 1) * 256, :]
+                .rearrange("p n i -> p (n i)")
+                .bitcast(F32)
+                .rearrange("p (n u) -> p n u", u=2),
+                in_=bank[:].rearrange("p (u n) -> p n u", u=2),
+            )
+
+        def mask_first(h):
             nc.vector.tensor_scalar(
-                out=parts[1][:, 0, n0:n1, :].rearrange("p n i -> p (n i)").bitcast(I32),
-                in0=w_raw[:, n0:n1, :].rearrange("p n i -> p (n i)").bitcast(I32),
+                out=hi32[h][:].bitcast(I32),
+                in0=w_first[h][:].bitcast(I32),
                 scalar1=HI_MASK,
                 scalar2=None,
                 op0=ALU.bitwise_and,
             )
 
-        def mask_rows(i0, i1):
-            nc.vector.tensor_scalar(
-                out=hi32[:, i0:i1, :].bitcast(I32),
-                in0=w_sb[0][:, i0:i1, :].bitcast(I32),
-                scalar1=-0x00100000,
-                scalar2=None,
-                op0=ALU.bitwise_and,
-            )
-
-        def cast_hi():
+        def cast_hi(h):
             nc.scalar.copy(
-                out=parts[0][:, 0, :, :].rearrange("p (c e) i -> p c i e", e=4),
-                in_=hi32[:].rearrange("p i (c e) -> p c i e", e=4),
+                out=parts[0][:, 0, h * 256 : (h + 1) * 256, :].rearrange("p (c e) i -> p c i e", e=4),
+                in_=hi32[h][:].rearrange("p i (c e) -> p c i e", e=4),
             )
 
-        def rest_w(a, n0, n1):
-            if a == 0:
-                hi = hi32[:, :, n0:n1].rearrange("p i (c e) -> p c i e", e=4)
-            else:
-                hi = parts[a][:, 0, n0:n1, :].rearrange("p (c e) i -> p c i e", e=4)
+        def rest_w(h):
             nc.vector.tensor_tensor(
-                out=parts[a][:, 1, n0:n1, :].rearrange("p (c e) i -> p c i e", e=4),
-                in0=w_sb[a][:, :, n0:n1].rearrange("p i (c e) -> p c i e", e=4),
-                in1=hi,
+                out=parts[0][:, 1, h * 256 : (h + 1) * 256, :].rearrange("p (c e) i -> p c i e", e=4),
+                in0=w_first[h][:].rearrange("p i (c e) -> p c i e", e=4),
+                in1=hi32[h][:].rearrange("p i (c e) -> p c i e", e=4),
                 op=ALU.subtract,
             )
 
-        def quantize_w(a, h):
+        def quantize_w(a):
             nc.vector.quantize_mx(
-                out=w_codes[a][:, h * M : (h + 1) * M].bitcast(FP8X4),
-                scales=w_scales[a][:, h * M : (h + 1) * M],
-                in_=parts[a][:, h, :, :].rearrange("p n i -> p (n i)"),
+                out=w_codes[a][:].bitcast(FP8X4),
+                scales=w_scales[a][:],
+                in_=parts[a][:].rearrange("p h n i -> p (h n i)"),
             )
 
         def gather(a, i, j0, c):
-            late = a == 1 and j0 >= FIRST
-            weights = wgt_late[:, j0 - FIRST : j0 - FIRST + c] if late else wgt_sb[:, j0 : j0 + c]
             nc.vector.tensor_tensor(
                 out=picked[a][:, i, j0 : j0 + c],
                 in0=planes[a][i][:].indirect(offsets[:, j0 // 16 : (j0 + c) // 16]),
-                in1=weights,
+                in1=wgt_sb[:, j0 : j0 + c],
                 op=ALU.mult,
             )
 
@@ -147,61 +173,50 @@ def tile_list_heads_tm_hl_bias_kernel(tc, xT, w, wgt, b, offs, out):
                 nc.vector.tensor_tensor(out=result[j][:], in0=acc[j][:], in1=bias[:], op=ALU.add)
                 nc.sync.dma_start(out=out[j * P : (j + 1) * P, :], in_=result[j][:])
 
-        load_w(0, 0, 2)
-        load_w(0, 2, 4)
-        load_w(1, 0, 4)
+        for h in range(2):
+            nc.sync.dma_start(out=w_first[h][:], in_=w_view[0][:, :, h * 256 : (h + 1) * 256])
         nc.sync.dma_start(offsets[:], offs)
-        nc.sync.dma_start(out=wgt_sb[:], in_=wgt)
-        for a, i in PLANE_ORDER:
+        nc.sync.dma_start(out=wgt_sb[:, 0:512], in_=wgt[:, 0:512])
+        load_plane(*PLANE_ORDER[0])
+        nc.sync.dma_start(out=wgt_sb[:, 512:S], in_=wgt[:, 512:S])
+        nc.sync.dma_start(out=w_second[:], in_=w_view[1])
+        for a, i in PLANE_ORDER[1:]:
             load_plane(a, i)
-        nc.sync.dma_start(out=wgt_late[:], in_=wgt[:, FIRST:S])
         nc.sync.dma_start(out=bias[:], in_=b.partition_broadcast(P))
 
-        mask_rows(0, 2)
-        mask_rows(2, 4)
-        rest_w(0, 0, 256)
-        rest_w(0, 256, 512)
-        cast_hi()
-        raw_w(0, 256)
-        raw_w(256, 512)
-        mask_packed(0, 256)
-        quantize_w(0, 1)
-        rest_w(1, 0, 256)
-        mask_packed(256, 512)
-        quantize_w(0, 0)
-        rest_w(1, 256, 512)
-        quantize_w(1, 0)
+        make_identity(nc, ident[:])
+        for h in range(2):
+            mask_first(h)
+            rest_w(h)
+            cast_hi(h)
         gather(0, 0, 0, 512)
-        quantize_w(1, 1)
+        quantize_w(0)
         gather(0, 0, 512, 512)
-        for i in (1, 2):
-            gather(0, i, 0, 512)
-            gather(0, i, 512, 512)
-        gather(1, 0, 0, 640)
-        gather(1, 1, 0, 640)
-        gather(0, 3, 0, 512)
-        interleave_x(0, 0, 256)
-        interleave_x(0, 256, 256)
-        gather(0, 3, 512, 512)
-        interleave_x(0, 512, 256)
-        interleave_x(0, 768, 256)
-        gather(1, 2, 0, 640)
-        quantize_x(0, 0, 256)
-        multiply(0, 0, 256)
-        gather(1, 3, 0, 640)
-        for j0 in (256, 512, 768):
-            quantize_x(0, j0, 256)
-            multiply(0, j0, 256)
-        for j0, c in ((0, 256), (256, 256), (512, 128)):
-            interleave_x(1, j0, c)
-        for i in range(3):
-            gather(1, i, 640, 384)
-        quantize_x(1, 0, 256)
-        multiply(1, 0, 256)
-        gather(1, 3, 640, 384)
-        interleave_x(1, 640, 256)
-        interleave_x(1, 896, 128)
-        for j0, c in ((256, 256), (512, 128), (640, 256), (896, 128)):
-            quantize_x(1, j0, c)
-            multiply(1, j0, c)
-        finish(0, 1024)
+        mask_negated()
+        gather(0, 1, 0, 1024)
+        for nb in range(M // P):
+            turn_rest(nb)
+        for h in range(2):
+            turn_back(h)
+        cast_negated(0, 512)
+        gather(0, 2, 0, 1024)
+        quantize_w(1)
+        gather(1, 0, 0, S)
+        gather(1, 1, 0, S)
+        for j0 in (0, 512):
+            gather(0, 3, j0, 512)
+            interleave_x(0, j0, PIECE)
+            interleave_x(0, j0 + PIECE, PIECE)
+        quantize_x(0, 0, PIECE)
+        multiply(0, 0, PIECE)
+        gather(1, 2, 0, S)
+        for j0 in range(PIECE, S, PIECE):
+            quantize_x(0, j0, PIECE)
+            multiply(0, j0, PIECE)
+        for j0 in range(0, S, PIECE):
+            gather(1, 3, j0, PIECE)
+            interleave_x(1, j0, PIECE)
+        for j0 in range(0, S, PIECE):
+            quantize_x(1, j0, PIECE)
+            multiply(1, j0, PIECE)
+        finish(0, S)

@@ -18,7 +18,7 @@ ACT = mybir.ActivationFunctionType
 
 FLOPS = 2 * 2 * K * M * S
 PIECE = 256
-PLANE_ORDER = ((0, 0), (0, 1), (0, 2), (1, 0), (1, 1), (0, 3), (1, 2), (1, 3))
+PLANE_ORDER = ((0, 0), (0, 1), (0, 2), (1, 0), (0, 3), (1, 1), (1, 2), (1, 3))
 HI_MASK = -0x00100000
 SIGN_BIT = -0x80000000
 
@@ -46,7 +46,9 @@ def tile_list_heads_tm_hl_bias_kernel(tc, xT, w, wgt, b, offs, out):
         w_codes = [keep.tile([P, 2 * M], U32, name=f"w_codes{a}", align_bytes=64) for a in range(PASSES)]
         w_scales = [keep.tile([P, 2 * M], U8, name=f"w_scales{a}", align_bytes=64) for a in range(PASSES)]
         hi32 = [keep.tile([P, PACK, M // 2], F32, name=f"hi32{h}") for h in range(2)]
-        picked = [keep.tile([P, PACK, S], F32, name=f"picked{a}") for a in range(PASSES)]
+        picked_flat = [keep.tile([P, PACK * S], F32, name=f"picked{a}", align_bytes=64) for a in range(PASSES)]
+        picked = [t[:].rearrange("p (i j) -> p i j", i=PACK) for t in picked_flat]
+        x_first = picked_flat[1][:, PACK * S - PIECE :].bitcast(BF16)
         x_bf = [keep.tile([P, S, PACK], BF16, name=f"x_bf{a}", align_bytes=64) for a in range(PASSES)]
         x_codes = [keep.tile([P, S], U32, name=f"x_codes{a}", align_bytes=64) for a in range(PASSES)]
         x_scales = [keep.tile([P, S], U8, name=f"x_scales{a}", align_bytes=64) for a in range(PASSES)]
@@ -146,11 +148,22 @@ def tile_list_heads_tm_hl_bias_kernel(tc, xT, w, wgt, b, offs, out):
                 in_=picked[a][:, :, j0 : j0 + c].rearrange("p i (c e) -> p c i e", e=4),
             )
 
+        def rounded(a, j0, c):
+            if a == 1 and j0 == 0:
+                return x_first.rearrange("p (j i) -> p j i", i=PACK)
+            return x_bf[a][:, j0 : j0 + c, :]
+
+        def interleave_pair(u, j0, c):
+            nc.scalar.copy(
+                out=rounded(1, j0, c)[:, :, 2 * u : 2 * u + 2].rearrange("p (c e) i -> p c i e", e=4),
+                in_=picked[1][:, 2 * u : 2 * u + 2, j0 : j0 + c].rearrange("p i (c e) -> p c i e", e=4),
+            )
+
         def quantize_x(a, j0, c):
             nc.vector.quantize_mx(
                 out=x_codes[a][:, j0 : j0 + c].bitcast(FP8X4),
                 scales=x_scales[a][:, j0 : j0 + c],
-                in_=x_bf[a][:, j0 : j0 + c, :].rearrange("p j i -> p (j i)"),
+                in_=rounded(a, j0, c).rearrange("p j i -> p (j i)"),
             )
 
         def multiply(a, j0, c):
@@ -202,21 +215,36 @@ def tile_list_heads_tm_hl_bias_kernel(tc, xT, w, wgt, b, offs, out):
         gather(0, 2, 0, 1024)
         quantize_w(1)
         gather(1, 0, 0, S)
-        gather(1, 1, 0, S)
         for j0 in (0, 512):
             gather(0, 3, j0, 512)
             interleave_x(0, j0, PIECE)
             interleave_x(0, j0 + PIECE, PIECE)
-        quantize_x(0, 0, PIECE)
-        multiply(0, 0, PIECE)
+        gather(1, 1, 0, S)
+        interleave_pair(0, 0, 128)
+        interleave_pair(0, 128, 384)
         gather(1, 2, 0, S)
-        for j0 in range(PIECE, S, PIECE):
+        for j0 in range(0, S, PIECE):
             quantize_x(0, j0, PIECE)
             multiply(0, j0, PIECE)
-        for j0 in range(0, S, PIECE):
-            gather(1, 3, j0, PIECE)
-            interleave_x(1, j0, PIECE)
-        for j0 in range(0, S, PIECE):
-            quantize_x(1, j0, PIECE)
-            multiply(1, j0, PIECE)
-        finish(0, S)
+        gather(1, 3, 0, 256)
+        interleave_pair(1, 0, 128)
+        interleave_pair(1, 128, 128)
+        gather(1, 3, 256, 512)
+        quantize_x(1, 0, 128)
+        multiply(1, 0, 128)
+        gather(1, 3, 768, 256)
+        interleave_pair(1, 256, 256)
+        interleave_x(1, 512, 256)
+        interleave_x(1, 768, 128)
+        interleave_x(1, 896, 128)
+        quantize_x(1, 128, 128)
+        multiply(1, 128, 128)
+        for j0, c in ((256, 256), (512, 256), (768, 128), (896, 128)):
+            quantize_x(1, j0, c)
+            multiply(1, j0, c)
+        finish(0, S - P)
+        last = S // P - 1
+        for n0 in (0, M // 2):
+            cols = slice(n0, n0 + M // 2)
+            nc.vector.tensor_tensor(out=result[last][:, cols], in0=acc[last][:, cols], in1=bias[:, cols], op=ALU.add)
+            nc.sync.dma_start(out=out[last * P :, cols], in_=result[last][:, cols])

@@ -18,6 +18,7 @@ ACT = mybir.ActivationFunctionType
 
 FLOPS = 2 * 2 * K * M * S
 PIECE = 256
+GROUPS = 8
 PLANE_ORDER = ((0, 0), (0, 1), (0, 2), (1, 0), (0, 3), (1, 1), (1, 2), (1, 3))
 HI_MASK = -0x00100000
 SIGN_BIT = -0x80000000
@@ -35,14 +36,21 @@ def tile_list_heads_tm_hl_bias_kernel(tc, xT, w, wgt, b, offs, out):
     ):
         offsets = lists.tile([P, S // 16], U16, name="offsets")
         wgt_sb = keep.tile([P, S], F32, name="wgt_sb")
+        wgt_rows = keep.tile([P, S], F32, name="wgt_rows")
+        wgt_turned = [
+            keep.tile([P, 4, GROUPS, P // GROUPS], F32, name=f"wgt_turned{h}", tag=f"turned{h}", align_bytes=64)
+            for h in range(2)
+        ]
+        first_lo = keep.tile([P, M, PACK], BF16, name="first_lo", align_bytes=64)
+        first_hi = []
         bias = keep.tile([P, M], F32, name="bias")
         planes = [[keep.tile([P, T], F32, name=f"plane{a}{i}") for i in range(PACK)] for a in range(PASSES)]
         w_first = [keep.tile([P, PACK, M // 2], F32, name=f"w_first{h}") for h in range(2)]
         w_second = keep.tile([P, PACK, M], F32, name="w_second")
         ident = keep.tile([P, P], F32, name="ident")
-        neg_hi = keep.tile([P, PACK, M], F32, name="neg_hi")
+        held = []
         lo_turned = keep.tile([P, M // P, 2, P, 2], BF16, name="lo_turned", align_bytes=64)
-        parts = [keep.tile([P, 2, M, PACK], BF16, name=f"parts{a}", align_bytes=64) for a in range(PASSES)]
+        parts = [None, keep.tile([P, 2, M, PACK], BF16, name="parts1", align_bytes=64)]
         w_codes = [keep.tile([P, 2 * M], U32, name=f"w_codes{a}", align_bytes=64) for a in range(PASSES)]
         w_scales = [keep.tile([P, 2 * M], U8, name=f"w_scales{a}", align_bytes=64) for a in range(PASSES)]
         hi32 = [keep.tile([P, PACK, M // 2], F32, name=f"hi32{h}") for h in range(2)]
@@ -58,9 +66,28 @@ def tile_list_heads_tm_hl_bias_kernel(tc, xT, w, wgt, b, offs, out):
         def load_plane(a, i):
             nc.sync.dma_start(out=planes[a][i][:], in_=x_view[a, i])
 
+        def spread_wgt(h):
+            turned, spread = acc[2 + h], acc[h]
+            for c in range(4):
+                at = (4 * h + c) * P
+                nc.tensor.transpose(turned[:, c * P : (c + 1) * P], wgt_rows[:, at : at + P], ident[:])
+            nc.scalar.copy(
+                out=wgt_turned[h][:],
+                in_=turned[:]
+                .rearrange("j (c q) -> j c q", c=4)[:, :, P - GROUPS :]
+                .unsqueeze(3)
+                .to_broadcast([P, 4, GROUPS, P // GROUPS]),
+            )
+            for c in range(4):
+                rows = wgt_turned[h][:, c, :, :].rearrange("j g r -> j (g r)")
+                nc.tensor.transpose(spread[:, c * P : (c + 1) * P], rows, ident[:])
+
+        def fetch_wgt(h):
+            nc.scalar.copy(out=wgt_sb[:, 512 * h : 512 * (h + 1)], in_=acc[h][:])
+
         def mask_negated():
             nc.vector.tensor_scalar(
-                out=neg_hi[:].bitcast(I32),
+                out=held[0][:].bitcast(I32),
                 in0=w_second[:].bitcast(I32),
                 scalar1=HI_MASK,
                 scalar2=SIGN_BIT,
@@ -71,18 +98,18 @@ def tile_list_heads_tm_hl_bias_kernel(tc, xT, w, wgt, b, offs, out):
         def cast_negated(n0, n1):
             nc.scalar.activation(
                 out=parts[1][:, 0, n0:n1, :].rearrange("p (c e) i -> p c i e", e=4),
-                in_=neg_hi[:, :, n0:n1].rearrange("p i (c e) -> p c i e", e=4),
+                in_=held[0][:, :, n0:n1].rearrange("p i (c e) -> p c i e", e=4),
                 func=ACT.Copy,
                 scale=-1.0,
             )
 
         def turn_rest(nb):
-            bank = acc[nb]
+            bank = acc[nb % 2]
             cols = slice(nb * P, (nb + 1) * P)
             for i in range(PACK):
                 target = bank[:, i * P : (i + 1) * P]
                 nc.tensor.matmul(target, lhsT=w_second[:, i, cols], rhs=ident[:], start=True, stop=False, is_transpose=True)
-                nc.tensor.matmul(target, lhsT=neg_hi[:, i, cols], rhs=ident[:], start=False, stop=True, is_transpose=True)
+                nc.tensor.matmul(target, lhsT=held[0][:, i, cols], rhs=ident[:], start=False, stop=True, is_transpose=True)
             nc.scalar.copy(
                 out=lo_turned[:, nb, :, :, :],
                 in_=bank[:].rearrange("n (u e p) -> n u p e", u=2, e=2),
@@ -115,13 +142,13 @@ def tile_list_heads_tm_hl_bias_kernel(tc, xT, w, wgt, b, offs, out):
 
         def cast_hi(h):
             nc.scalar.copy(
-                out=parts[0][:, 0, h * 256 : (h + 1) * 256, :].rearrange("p (c e) i -> p c i e", e=4),
+                out=first_hi[0][:, h * 256 : (h + 1) * 256, :].rearrange("p (c e) i -> p c i e", e=4),
                 in_=hi32[h][:].rearrange("p i (c e) -> p c i e", e=4),
             )
 
         def rest_w(h):
             nc.vector.tensor_tensor(
-                out=parts[0][:, 1, h * 256 : (h + 1) * 256, :].rearrange("p (c e) i -> p c i e", e=4),
+                out=first_lo[:, h * 256 : (h + 1) * 256, :].rearrange("p (c e) i -> p c i e", e=4),
                 in0=w_first[h][:].rearrange("p i (c e) -> p c i e", e=4),
                 in1=hi32[h][:].rearrange("p i (c e) -> p c i e", e=4),
                 op=ALU.subtract,
@@ -132,6 +159,13 @@ def tile_list_heads_tm_hl_bias_kernel(tc, xT, w, wgt, b, offs, out):
                 out=w_codes[a][:].bitcast(FP8X4),
                 scales=w_scales[a][:],
                 in_=parts[a][:].rearrange("p h n i -> p (h n i)"),
+            )
+
+        def quantize_first(k, part):
+            nc.vector.quantize_mx(
+                out=w_codes[0][:, k * M : (k + 1) * M].bitcast(FP8X4),
+                scales=w_scales[0][:, k * M : (k + 1) * M],
+                in_=part[:].rearrange("p n i -> p (n i)"),
             )
 
         def gather(a, i, j0, c):
@@ -186,26 +220,32 @@ def tile_list_heads_tm_hl_bias_kernel(tc, xT, w, wgt, b, offs, out):
                 nc.vector.tensor_tensor(out=result[j][:], in0=acc[j][:], in1=bias[:], op=ALU.add)
                 nc.sync.dma_start(out=out[j * P : (j + 1) * P, :], in_=result[j][:])
 
+        nc.sync.dma_start(out=wgt_rows[P - GROUPS :, :], in_=wgt[0 : P : P // GROUPS, :])
         for h in range(2):
             nc.sync.dma_start(out=w_first[h][:], in_=w_view[0][:, :, h * 256 : (h + 1) * 256])
         nc.sync.dma_start(offsets[:], offs)
-        nc.sync.dma_start(out=wgt_sb[:, 0:512], in_=wgt[:, 0:512])
-        load_plane(*PLANE_ORDER[0])
-        nc.sync.dma_start(out=wgt_sb[:, 512:S], in_=wgt[:, 512:S])
         nc.sync.dma_start(out=w_second[:], in_=w_view[1])
-        for a, i in PLANE_ORDER[1:]:
+        for a, i in PLANE_ORDER:
             load_plane(a, i)
         nc.sync.dma_start(out=bias[:], in_=b.partition_broadcast(P))
 
         make_identity(nc, ident[:])
+        nc.vector.memset(wgt_rows[0 : P - GROUPS, :], 0.0)
+        for h in range(2):
+            spread_wgt(h)
+        fetch_wgt(0)
         for h in range(2):
             mask_first(h)
             rest_w(h)
+        first_hi.append(keep.tile([P, M, PACK], BF16, name="first_hi", tag="turned0", align_bytes=64))
+        for h in range(2):
             cast_hi(h)
-        gather(0, 0, 0, 512)
-        quantize_w(0)
-        gather(0, 0, 512, 512)
+        fetch_wgt(1)
+        quantize_first(1, first_lo)
+        held.append(keep.tile([P, PACK, M], F32, name="neg_hi", tag="turned1", align_bytes=64))
         mask_negated()
+        quantize_first(0, first_hi[0])
+        gather(0, 0, 0, S)
         gather(0, 1, 0, 1024)
         for nb in range(M // P):
             turn_rest(nb)

@@ -5,6 +5,9 @@ K, M, T, S = 1024, 512, 2048, 1024
 P = 128
 PACK = 4
 PASSES = K // (P * PACK)
+GROUPS = 8
+PER_OFFSET_COLUMN = 16
+RUN = 4
 
 F32 = mybir.dt.float32
 BF16 = mybir.dt.bfloat16
@@ -17,11 +20,15 @@ ALU = mybir.AluOpType
 ACT = mybir.ActivationFunctionType
 
 FLOPS = 2 * 2 * K * M * S
-PIECE = 256
-GROUPS = 8
-PLANE_ORDER = ((0, 0), (0, 1), (0, 2), (1, 0), (0, 3), (1, 1), (1, 2), (1, 3))
 HI_MASK = -0x00100000
 SIGN_BIT = -0x80000000
+
+HALF_S = S // 2
+HALF_M = M // 2
+PART = M * PACK
+WGT_ROW0 = P - 2 * GROUPS
+PIECE = 2 * P
+PLANE_ORDER = ((0, 0), (0, 1), (0, 2), (1, 0), (0, 3), (1, 1), (1, 2), (1, 3))
 
 
 def tile_list_heads_tm_hl_bias_kernel(tc, xT, w, wgt, b, offs, out):
@@ -34,60 +41,94 @@ def tile_list_heads_tm_hl_bias_kernel(tc, xT, w, wgt, b, offs, out):
         tc.tile_pool(name="keep", bufs=1) as keep,
         tc.psum_pool(name="psum", bufs=1) as psum,
     ):
-        offsets = lists.tile([P, S // 16], U16, name="offsets")
+        offsets = lists.tile([P, S // PER_OFFSET_COLUMN], U16, name="offsets")
         wgt_sb = keep.tile([P, S], F32, name="wgt_sb")
-        wgt_rows = keep.tile([P, S], F32, name="wgt_rows")
-        wgt_turned = [
-            keep.tile([P, 4, GROUPS, P // GROUPS], F32, name=f"wgt_turned{h}", tag=f"turned{h}", align_bytes=64)
-            for h in range(2)
-        ]
-        first_lo = keep.tile([P, M, PACK], BF16, name="first_lo", align_bytes=64)
-        first_hi = []
+        wgt_rows = keep.tile([P, HALF_S], F32, name="wgt_rows")
+        room = keep.tile([P, 4 * PART], BF16, name="room", align_bytes=64)
+        first_lo, first_hi, second_hi, second_lo = (
+            room[:, part * PART : (part + 1) * PART].rearrange("p (n i) -> p n i", i=PACK) for part in range(4)
+        )
+        turned_at = PART + PART // 2 - 2 * P
+        turned = room[:, turned_at : turned_at + 2 * S].bitcast(F32)
         bias = keep.tile([P, M], F32, name="bias")
         planes = [[keep.tile([P, T], F32, name=f"plane{a}{i}") for i in range(PACK)] for a in range(PASSES)]
-        w_first = [keep.tile([P, PACK, M // 2], F32, name=f"w_first{h}") for h in range(2)]
+        w_first = [keep.tile([P, PACK, HALF_M], F32, name=f"w_first{h}") for h in range(2)]
         w_second = keep.tile([P, PACK, M], F32, name="w_second")
         ident = keep.tile([P, P], F32, name="ident")
-        held = []
+        neg_hi = keep.tile([P, PACK, M], F32, name="neg_hi")
         lo_turned = keep.tile([P, M // P, 2, P, 2], BF16, name="lo_turned", align_bytes=64)
-        parts = [None, keep.tile([P, 2, M, PACK], BF16, name="parts1", align_bytes=64)]
         w_codes = [keep.tile([P, 2 * M], U32, name=f"w_codes{a}", align_bytes=64) for a in range(PASSES)]
         w_scales = [keep.tile([P, 2 * M], U8, name=f"w_scales{a}", align_bytes=64) for a in range(PASSES)]
-        hi32 = [keep.tile([P, PACK, M // 2], F32, name=f"hi32{h}") for h in range(2)]
+        hi32 = keep.tile([P, PACK, M], F32, name="hi32")
         picked_flat = [keep.tile([P, PACK * S], F32, name=f"picked{a}", align_bytes=64) for a in range(PASSES)]
-        picked = [t[:].rearrange("p (i j) -> p i j", i=PACK) for t in picked_flat]
-        x_first = picked_flat[1][:, PACK * S - PIECE :].bitcast(BF16)
+        picked = [flat[:].rearrange("p (i j) -> p i j", i=PACK) for flat in picked_flat]
+        x_first = picked_flat[1][:, PACK * S - PIECE :].bitcast(BF16).rearrange("p (j i) -> p j i", i=PACK)
         x_bf = [keep.tile([P, S, PACK], BF16, name=f"x_bf{a}", align_bytes=64) for a in range(PASSES)]
         x_codes = [keep.tile([P, S], U32, name=f"x_codes{a}", align_bytes=64) for a in range(PASSES)]
         x_scales = [keep.tile([P, S], U8, name=f"x_scales{a}", align_bytes=64) for a in range(PASSES)]
         acc = [psum.tile([P, M], F32, name=f"acc{j}") for j in range(S // P)]
         result = [keep.tile([P, M], F32, name=f"result{j}") for j in range(S // P)]
 
-        def load_plane(a, i):
-            nc.sync.dma_start(out=planes[a][i][:], in_=x_view[a, i])
+        def by_runs(tile_view, axes):
+            return tile_view.rearrange(axes + " -> p c i e", e=RUN)
+
+        def interleaved(tile_view):
+            return by_runs(tile_view, "p (c e) i")
+
+        def planar(tile_view):
+            return by_runs(tile_view, "p i (c e)")
+
+
+        def turn_wgt(v):
+            bank = acc[2 + v]
+            for u in range(2):
+                at = (2 * v + u) * P
+                nc.tensor.transpose(bank[:, u * P : (u + 1) * P], wgt_rows[:, at : at + P], ident[:])
+            nc.scalar.copy(
+                out=turned.rearrange("j (h u g r) -> j h u g r", h=2, u=4, g=GROUPS)[:, :, 2 * v : 2 * v + 2, :, :],
+                in_=bank[:, 0 : 2 * P]
+                .rearrange("j (u q) -> j u q", u=2)[:, :, WGT_ROW0:]
+                .rearrange("j u (g h) -> j h u g", h=2)
+                .unsqueeze(4)
+                .to_broadcast([P, 2, 2, GROUPS, P // GROUPS]),
+            )
 
         def spread_wgt(h):
-            turned, spread = acc[2 + h], acc[h]
-            for c in range(4):
-                at = (4 * h + c) * P
-                nc.tensor.transpose(turned[:, c * P : (c + 1) * P], wgt_rows[:, at : at + P], ident[:])
-            nc.scalar.copy(
-                out=wgt_turned[h][:],
-                in_=turned[:]
-                .rearrange("j (c q) -> j c q", c=4)[:, :, P - GROUPS :]
-                .unsqueeze(3)
-                .to_broadcast([P, 4, GROUPS, P // GROUPS]),
-            )
-            for c in range(4):
-                rows = wgt_turned[h][:, c, :, :].rearrange("j g r -> j (g r)")
-                nc.tensor.transpose(spread[:, c * P : (c + 1) * P], rows, ident[:])
+            for block in range(HALF_S // P):
+                at = h * HALF_S + block * P
+                nc.tensor.transpose(acc[h][:, block * P : (block + 1) * P], turned[:, at : at + P], ident[:])
 
         def fetch_wgt(h):
-            nc.scalar.copy(out=wgt_sb[:, 512 * h : 512 * (h + 1)], in_=acc[h][:])
+            nc.scalar.copy(out=wgt_sb[:, h * HALF_S : (h + 1) * HALF_S], in_=acc[h][:])
 
-        def mask_negated():
+
+        def mask_first(h, n0):
+            at = h * HALF_M + n0
             nc.vector.tensor_scalar(
-                out=held[0][:].bitcast(I32),
+                out=hi32[:, :, at : at + P].bitcast(I32),
+                in0=w_first[h][:, :, n0 : n0 + P].bitcast(I32),
+                scalar1=HI_MASK,
+                scalar2=None,
+                op0=ALU.bitwise_and,
+            )
+
+        def subtract_first(h, n0):
+            at = h * HALF_M + n0
+            nc.vector.tensor_tensor(
+                out=interleaved(first_lo[:, at : at + P, :]),
+                in0=planar(w_first[h][:, :, n0 : n0 + P]),
+                in1=planar(hi32[:, :, at : at + P]),
+                op=ALU.subtract,
+            )
+
+        def cast_first(h):
+            cols = slice(h * HALF_M, (h + 1) * HALF_M)
+            nc.scalar.copy(out=interleaved(first_hi[:, cols, :]), in_=planar(hi32[:, :, cols]))
+
+
+        def mask_second():
+            nc.vector.tensor_scalar(
+                out=neg_hi[:].bitcast(I32),
                 in0=w_second[:].bitcast(I32),
                 scalar1=HI_MASK,
                 scalar2=SIGN_BIT,
@@ -95,196 +136,163 @@ def tile_list_heads_tm_hl_bias_kernel(tc, xT, w, wgt, b, offs, out):
                 op1=ALU.bitwise_xor,
             )
 
-        def cast_negated(n0, n1):
-            nc.scalar.activation(
-                out=parts[1][:, 0, n0:n1, :].rearrange("p (c e) i -> p c i e", e=4),
-                in_=held[0][:, :, n0:n1].rearrange("p i (c e) -> p c i e", e=4),
-                func=ACT.Copy,
-                scale=-1.0,
-            )
+        def cast_second():
+            nc.scalar.activation(out=interleaved(second_hi), in_=planar(neg_hi[:]), func=ACT.Copy, scale=-1.0)
 
-        def turn_rest(nb):
-            bank = acc[nb % 2]
+        def turn_lo(nb):
+            bank = acc[(nb + 2) % 4]
             cols = slice(nb * P, (nb + 1) * P)
             for i in range(PACK):
                 target = bank[:, i * P : (i + 1) * P]
-                nc.tensor.matmul(target, lhsT=w_second[:, i, cols], rhs=ident[:], start=True, stop=False, is_transpose=True)
-                nc.tensor.matmul(target, lhsT=held[0][:, i, cols], rhs=ident[:], start=False, stop=True, is_transpose=True)
+                for source, is_first in ((w_second, True), (neg_hi, False)):
+                    nc.tensor.matmul(
+                        target,
+                        lhsT=source[:, i, cols],
+                        rhs=ident[:],
+                        start=is_first,
+                        stop=not is_first,
+                        is_transpose=True,
+                    )
             nc.scalar.copy(
                 out=lo_turned[:, nb, :, :, :],
                 in_=bank[:].rearrange("n (u e p) -> n u p e", u=2, e=2),
             )
 
-        def turn_back(h):
+        def turn_lo_back(h):
             bank = acc[4 + h]
             words = lo_turned[:].rearrange("n b u p e -> n (b u p e)").bitcast(F32)
             for u in range(2):
-                for b2 in range(2):
-                    at = ((2 * h + b2) * 2 + u) * P
-                    to = (2 * u + b2) * P
+                for block in range(2):
+                    at = ((2 * h + block) * 2 + u) * P
+                    to = (2 * u + block) * P
                     nc.tensor.transpose(bank[:, to : to + P], words[:, at : at + P], ident[:])
             nc.scalar.copy(
-                out=parts[1][:, 1, h * 256 : (h + 1) * 256, :]
+                out=second_lo[:, h * HALF_M : (h + 1) * HALF_M, :]
                 .rearrange("p n i -> p (n i)")
                 .bitcast(F32)
                 .rearrange("p (n u) -> p n u", u=2),
                 in_=bank[:].rearrange("p (u n) -> p n u", u=2),
             )
 
-        def mask_first(h):
-            nc.vector.tensor_scalar(
-                out=hi32[h][:].bitcast(I32),
-                in0=w_first[h][:].bitcast(I32),
-                scalar1=HI_MASK,
-                scalar2=None,
-                op0=ALU.bitwise_and,
-            )
-
-        def cast_hi(h):
-            nc.scalar.copy(
-                out=first_hi[0][:, h * 256 : (h + 1) * 256, :].rearrange("p (c e) i -> p c i e", e=4),
-                in_=hi32[h][:].rearrange("p i (c e) -> p c i e", e=4),
-            )
-
-        def rest_w(h):
-            nc.vector.tensor_tensor(
-                out=first_lo[:, h * 256 : (h + 1) * 256, :].rearrange("p (c e) i -> p c i e", e=4),
-                in0=w_first[h][:].rearrange("p i (c e) -> p c i e", e=4),
-                in1=hi32[h][:].rearrange("p i (c e) -> p c i e", e=4),
-                op=ALU.subtract,
-            )
-
         def quantize_w(a):
             nc.vector.quantize_mx(
                 out=w_codes[a][:].bitcast(FP8X4),
                 scales=w_scales[a][:],
-                in_=parts[a][:].rearrange("p h n i -> p (h n i)"),
+                in_=room[:, 2 * PART * a : 2 * PART * (a + 1)],
             )
 
-        def quantize_first(k, part):
-            nc.vector.quantize_mx(
-                out=w_codes[0][:, k * M : (k + 1) * M].bitcast(FP8X4),
-                scales=w_scales[0][:, k * M : (k + 1) * M],
-                in_=part[:].rearrange("p n i -> p (n i)"),
-            )
 
         def gather(a, i, j0, c):
             nc.vector.tensor_tensor(
                 out=picked[a][:, i, j0 : j0 + c],
-                in0=planes[a][i][:].indirect(offsets[:, j0 // 16 : (j0 + c) // 16]),
+                in0=planes[a][i][:].indirect(offsets[:, j0 // PER_OFFSET_COLUMN : (j0 + c) // PER_OFFSET_COLUMN]),
                 in1=wgt_sb[:, j0 : j0 + c],
                 op=ALU.mult,
             )
 
-        def interleave_x(a, j0, c):
-            nc.scalar.copy(
-                out=x_bf[a][:, j0 : j0 + c, :].rearrange("p (c e) i -> p c i e", e=4),
-                in_=picked[a][:, :, j0 : j0 + c].rearrange("p i (c e) -> p c i e", e=4),
-            )
-
         def rounded(a, j0, c):
             if a == 1 and j0 == 0:
-                return x_first.rearrange("p (j i) -> p j i", i=PACK)
+                return x_first
             return x_bf[a][:, j0 : j0 + c, :]
 
-        def interleave_pair(u, j0, c):
-            nc.scalar.copy(
-                out=rounded(1, j0, c)[:, :, 2 * u : 2 * u + 2].rearrange("p (c e) i -> p c i e", e=4),
-                in_=picked[1][:, 2 * u : 2 * u + 2, j0 : j0 + c].rearrange("p i (c e) -> p c i e", e=4),
-            )
+        def round_all(a, j0, c):
+            nc.scalar.copy(out=interleaved(rounded(a, j0, c)), in_=planar(picked[a][:, :, j0 : j0 + c]))
 
-        def quantize_x(a, j0, c):
+        def round_pair(u, j0, c):
+            pair = slice(2 * u, 2 * u + 2)
+            nc.scalar.copy(out=interleaved(rounded(1, j0, c)[:, :, pair]), in_=planar(picked[1][:, pair, j0 : j0 + c]))
+
+        def multiply(a, j0, c):
             nc.vector.quantize_mx(
                 out=x_codes[a][:, j0 : j0 + c].bitcast(FP8X4),
                 scales=x_scales[a][:, j0 : j0 + c],
                 in_=rounded(a, j0, c).rearrange("p j i -> p (j i)"),
             )
-
-        def multiply(a, j0, c):
             for j in range(j0 // P, (j0 + c) // P):
                 cols = slice(j * P, (j + 1) * P)
-                for k in range(2):
-                    w_cols = slice(k * M, (k + 1) * M)
+                for part in range(2):
+                    w_cols = slice(part * M, (part + 1) * M)
                     nc.tensor.matmul_mx(
                         out=acc[j][:],
                         lhsT=x_codes[a][:, cols].bitcast(FP8X4),
                         lhsT_scale=x_scales[a][:, cols],
                         rhs=w_codes[a][:, w_cols].bitcast(FP8X4),
                         rhs_scale=w_scales[a][:, w_cols],
-                        start=(a == 0 and k == 0),
-                        stop=(a == PASSES - 1 and k == 1),
+                        start=(a == 0 and part == 0),
+                        stop=(a == PASSES - 1 and part == 1),
                     )
 
-        def finish(j0, c):
-            for j in range(j0 // P, (j0 + c) // P):
-                nc.vector.tensor_tensor(out=result[j][:], in0=acc[j][:], in1=bias[:], op=ALU.add)
-                nc.sync.dma_start(out=out[j * P : (j + 1) * P, :], in_=result[j][:])
+        def finish(j, n0, n1):
+            nc.vector.tensor_tensor(out=result[j][:, n0:n1], in0=acc[j][:, n0:n1], in1=bias[:, n0:n1], op=ALU.add)
+            nc.sync.dma_start(out=out[j * P : (j + 1) * P, n0:n1], in_=result[j][:, n0:n1])
 
-        nc.sync.dma_start(out=wgt_rows[P - GROUPS :, :], in_=wgt[0 : P : P // GROUPS, :])
         for h in range(2):
-            nc.sync.dma_start(out=w_first[h][:], in_=w_view[0][:, :, h * 256 : (h + 1) * 256])
+            nc.sync.dma_start(
+                out=wgt_rows[WGT_ROW0 + h : P : 2, :],
+                in_=wgt[0 : P : P // GROUPS, h * HALF_S : (h + 1) * HALF_S],
+            )
+        for h in range(2):
+            nc.sync.dma_start(out=w_first[h][:], in_=w_view[0][:, :, h * HALF_M : (h + 1) * HALF_M])
         nc.sync.dma_start(offsets[:], offs)
         nc.sync.dma_start(out=w_second[:], in_=w_view[1])
         for a, i in PLANE_ORDER:
-            load_plane(a, i)
+            nc.sync.dma_start(out=planes[a][i][:], in_=x_view[a, i])
         nc.sync.dma_start(out=bias[:], in_=b.partition_broadcast(P))
 
-        make_identity(nc, ident[:])
-        nc.vector.memset(wgt_rows[0 : P - GROUPS, :], 0.0)
+        nc.vector.memset(ident[:], 0.0)
+        make_identity(nc, ident[:], nomemset=True)
+        nc.vector.memset(wgt_rows[0:WGT_ROW0, :], 0.0)
+        for v in range(2):
+            turn_wgt(v)
         for h in range(2):
             spread_wgt(h)
-        fetch_wgt(0)
         for h in range(2):
-            mask_first(h)
-            rest_w(h)
-        first_hi.append(keep.tile([P, M, PACK], BF16, name="first_hi", tag="turned0", align_bytes=64))
+            for n0 in (0, P):
+                mask_first(h, n0)
+            for n0 in (0, P):
+                subtract_first(h, n0)
         for h in range(2):
-            cast_hi(h)
-        fetch_wgt(1)
-        quantize_first(1, first_lo)
-        held.append(keep.tile([P, PACK, M], F32, name="neg_hi", tag="turned1", align_bytes=64))
-        mask_negated()
-        quantize_first(0, first_hi[0])
+            cast_first(h)
+        for h in range(2):
+            fetch_wgt(h)
+        mask_second()
+        quantize_w(0)
+
         gather(0, 0, 0, S)
-        gather(0, 1, 0, 1024)
+        gather(0, 1, 0, S)
         for nb in range(M // P):
-            turn_rest(nb)
+            turn_lo(nb)
         for h in range(2):
-            turn_back(h)
-        cast_negated(0, 512)
-        gather(0, 2, 0, 1024)
+            turn_lo_back(h)
+        cast_second()
+        gather(0, 2, 0, S)
         quantize_w(1)
         gather(1, 0, 0, S)
-        for j0 in (0, 512):
-            gather(0, 3, j0, 512)
-            interleave_x(0, j0, PIECE)
-            interleave_x(0, j0 + PIECE, PIECE)
+        for j0 in (0, HALF_S):
+            gather(0, 3, j0, HALF_S)
+            round_all(0, j0, PIECE)
+            round_all(0, j0 + PIECE, PIECE)
         gather(1, 1, 0, S)
-        interleave_pair(0, 0, 128)
-        interleave_pair(0, 128, 384)
+        round_pair(0, 0, P)
+        round_pair(0, P, HALF_S - P)
         gather(1, 2, 0, S)
         for j0 in range(0, S, PIECE):
-            quantize_x(0, j0, PIECE)
             multiply(0, j0, PIECE)
-        gather(1, 3, 0, 256)
-        interleave_pair(1, 0, 128)
-        interleave_pair(1, 128, 128)
-        gather(1, 3, 256, 512)
-        quantize_x(1, 0, 128)
-        multiply(1, 0, 128)
-        gather(1, 3, 768, 256)
-        interleave_pair(1, 256, 256)
-        interleave_x(1, 512, 256)
-        interleave_x(1, 768, 128)
-        interleave_x(1, 896, 128)
-        quantize_x(1, 128, 128)
-        multiply(1, 128, 128)
-        for j0, c in ((256, 256), (512, 256), (768, 128), (896, 128)):
-            quantize_x(1, j0, c)
+
+        gather(1, 3, 0, PIECE)
+        round_pair(1, 0, P)
+        round_pair(1, P, P)
+        gather(1, 3, PIECE, S - 2 * PIECE)
+        multiply(1, 0, P)
+        gather(1, 3, S - PIECE, PIECE)
+        round_pair(1, PIECE, PIECE)
+        round_all(1, HALF_S, PIECE)
+        round_all(1, S - 2 * P, P)
+        round_all(1, S - P, P)
+        for j0, c in ((P, P), (PIECE, PIECE), (HALF_S, PIECE), (S - 2 * P, P), (S - P, P)):
             multiply(1, j0, c)
-        finish(0, S - P)
         last = S // P - 1
-        for n0 in (0, M // 2):
-            cols = slice(n0, n0 + M // 2)
-            nc.vector.tensor_tensor(out=result[last][:, cols], in0=acc[last][:, cols], in1=bias[:, cols], op=ALU.add)
-            nc.sync.dma_start(out=out[last * P :, cols], in_=result[last][:, cols])
+        for j in range(last):
+            finish(j, 0, M)
+        for n0 in (0, HALF_M):
+            finish(last, n0, n0 + HALF_M)

@@ -63,6 +63,7 @@ def tile_list_heads_tm_hl_bias_kernel(tc, xT, w, wgt, b, offs, out):
         picked_flat = [keep.tile([P, PACK * S], F32, name=f"picked{a}", align_bytes=64) for a in range(PASSES)]
         picked = [flat[:].rearrange("p (i j) -> p i j", i=PACK) for flat in picked_flat]
         x_first = picked_flat[1][:, PACK * S - PIECE :].bitcast(BF16).rearrange("p (j i) -> p j i", i=PACK)
+        x_early = picked_flat[1][:, S : S + PIECE].bitcast(BF16).rearrange("p (j i) -> p j i", i=PACK)
         x_bf = [keep.tile([P, S, PACK], BF16, name=f"x_bf{a}", align_bytes=64) for a in range(PASSES)]
         x_codes = [keep.tile([P, S], U32, name=f"x_codes{a}", align_bytes=64) for a in range(PASSES)]
         x_scales = [keep.tile([P, S], U8, name=f"x_scales{a}", align_bytes=64) for a in range(PASSES)]
@@ -191,8 +192,8 @@ def tile_list_heads_tm_hl_bias_kernel(tc, xT, w, wgt, b, offs, out):
             )
 
         def rounded(a, j0, c):
-            if a == 1 and j0 == 0:
-                return x_first
+            if j0 == 0:
+                return x_first if a == 1 else x_early
             return x_bf[a][:, j0 : j0 + c, :]
 
         def round_all(a, j0, c):
@@ -270,13 +271,15 @@ def tile_list_heads_tm_hl_bias_kernel(tc, xT, w, wgt, b, offs, out):
         gather(1, 0, 0, S)
         for j0 in (0, HALF_S):
             gather(0, 3, j0, HALF_S)
-            round_all(0, j0, PIECE)
-            round_all(0, j0 + PIECE, PIECE)
+        for j0, c in ((0, P), (P, P), (PIECE, PIECE), (HALF_S, PIECE), (S - PIECE, PIECE)):
+            round_all(0, j0, c)
+        multiply(0, 0, P)
+        multiply(0, P, P)
         gather(1, 1, 0, S)
         round_pair(0, 0, P)
         round_pair(0, P, HALF_S - P)
         gather(1, 2, 0, S)
-        for j0 in range(0, S, PIECE):
+        for j0 in range(PIECE, S, PIECE):
             multiply(0, j0, PIECE)
 
         gather(1, 3, 0, PIECE)

@@ -64,6 +64,7 @@ def tile_list_heads_tm_hl_bias_kernel(tc, xT, w, wgt, b, offs, out):
         picked = [flat[:].rearrange("p (i j) -> p i j", i=PACK) for flat in picked_flat]
         x_first = picked_flat[1][:, PACK * S - PIECE :].bitcast(BF16).rearrange("p (j i) -> p j i", i=PACK)
         x_early = picked_flat[1][:, S : S + PIECE].bitcast(BF16).rearrange("p (j i) -> p j i", i=PACK)
+        x_middle = picked_flat[1][:, 2 * S : 2 * S + PIECE].bitcast(BF16).rearrange("p (j i) -> p j i", i=PACK)
         x_bf = [keep.tile([P, S, PACK], BF16, name=f"x_bf{a}", align_bytes=64) for a in range(PASSES)]
         x_codes = [keep.tile([P, S], U32, name=f"x_codes{a}", align_bytes=64) for a in range(PASSES)]
         x_scales = [keep.tile([P, S], U8, name=f"x_scales{a}", align_bytes=64) for a in range(PASSES)]
@@ -194,6 +195,8 @@ def tile_list_heads_tm_hl_bias_kernel(tc, xT, w, wgt, b, offs, out):
         def rounded(a, j0, c):
             if j0 == 0:
                 return x_first if a == 1 else x_early
+            if a == 0 and j0 == HALF_S:
+                return x_middle
             return x_bf[a][:, j0 : j0 + c, :]
 
         def round_all(a, j0, c):
@@ -227,11 +230,8 @@ def tile_list_heads_tm_hl_bias_kernel(tc, xT, w, wgt, b, offs, out):
             nc.vector.tensor_tensor(out=result[j][:, n0:n1], in0=acc[j][:, n0:n1], in1=bias[:, n0:n1], op=ALU.add)
             nc.sync.dma_start(out=out[j * P : (j + 1) * P, n0:n1], in_=result[j][:, n0:n1])
 
-        for h in range(2):
-            nc.sync.dma_start(
-                out=wgt_rows[WGT_ROW0 + h : P : 2, :],
-                in_=wgt[0 : P : P // GROUPS, h * HALF_S : (h + 1) * HALF_S],
-            )
+        half_rows = wgt.rearrange("p (h c) -> (p h) c", h=2)
+        nc.sync.dma_start(out=wgt_rows[WGT_ROW0:P, :], in_=half_rows[0 : 2 * P : 2 * GROUPS + 1, :])
         for h in range(2):
             nc.sync.dma_start(out=w_first[h][:], in_=w_view[0][:, :, h * HALF_M : (h + 1) * HALF_M])
         nc.sync.dma_start(offsets[:], offs)
@@ -271,16 +271,17 @@ def tile_list_heads_tm_hl_bias_kernel(tc, xT, w, wgt, b, offs, out):
         gather(1, 0, 0, S)
         for j0 in (0, HALF_S):
             gather(0, 3, j0, HALF_S)
-        for j0, c in ((0, P), (P, P), (PIECE, PIECE), (HALF_S, PIECE), (S - PIECE, PIECE)):
+        for j0, c in ((0, P), (P, P), (PIECE, PIECE), (HALF_S, P), (HALF_S + P, P), (S - PIECE, PIECE)):
             round_all(0, j0, c)
         multiply(0, 0, P)
         multiply(0, P, P)
         gather(1, 1, 0, S)
+        for j0, c in ((PIECE, PIECE), (HALF_S, P), (HALF_S + P, P)):
+            multiply(0, j0, c)
         round_pair(0, 0, P)
         round_pair(0, P, HALF_S - P)
         gather(1, 2, 0, S)
-        for j0 in range(PIECE, S, PIECE):
-            multiply(0, j0, PIECE)
+        multiply(0, S - PIECE, PIECE)
 
         gather(1, 3, 0, PIECE)
         round_pair(1, 0, P)

@@ -42,34 +42,34 @@ def tile_list_heads_tm_hl_bias_kernel(tc, xT, w, wgt, b, offs, out):
         tc.psum_pool(name="psum", bufs=1) as psum,
     ):
         offsets = lists.tile([P, S // PER_OFFSET_COLUMN], U16, name="offsets")
-        wgt_sb = keep.tile([P, S], F32, name="wgt_sb")
-        wgt_rows = keep.tile([P, HALF_S], F32, name="wgt_rows")
-        room = keep.tile([P, 4 * PART], BF16, name="room", align_bytes=64)
+        wgt_sb = keep.tile([P, S], F32, name="wgt_sb", align_bytes=256)
+        wgt_rows = keep.tile([P, HALF_S], F32, name="wgt_rows", align_bytes=256)
+        room = keep.tile([P, 4 * PART], BF16, name="room", align_bytes=256)
         first_lo, first_hi, second_hi, second_lo = (
             room[:, part * PART : (part + 1) * PART].rearrange("p (n i) -> p n i", i=PACK) for part in range(4)
         )
         turned_at = PART + PART // 2 - 2 * P
         turned = room[:, turned_at : turned_at + 2 * S].bitcast(F32)
-        bias = keep.tile([P, M], F32, name="bias")
-        planes = [[keep.tile([P, T], F32, name=f"plane{a}{i}") for i in range(PACK)] for a in range(PASSES)]
-        w_first = [keep.tile([P, PACK, HALF_M], F32, name=f"w_first{h}") for h in range(2)]
-        w_second = keep.tile([P, PACK, M], F32, name="w_second")
-        ident = keep.tile([P, P], F32, name="ident")
-        neg_hi = keep.tile([P, PACK, M], F32, name="neg_hi")
-        lo_turned = keep.tile([P, M // P, 2, P, 2], BF16, name="lo_turned", align_bytes=64)
-        w_codes = [keep.tile([P, 2 * M], U32, name=f"w_codes{a}", align_bytes=64) for a in range(PASSES)]
-        w_scales = [keep.tile([P, 2 * M], U8, name=f"w_scales{a}", align_bytes=64) for a in range(PASSES)]
-        hi32 = keep.tile([P, PACK, M], F32, name="hi32")
-        picked_flat = [keep.tile([P, PACK * S], F32, name=f"picked{a}", align_bytes=64) for a in range(PASSES)]
-        picked = [flat[:].rearrange("p (i j) -> p i j", i=PACK) for flat in picked_flat]
+        bias = keep.tile([P, M], F32, name="bias", align_bytes=256)
+        planes = [[keep.tile([P, T], F32, name=f"plane{a}{i}", align_bytes=256) for i in range(PACK)] for a in range(PASSES)]
+        w_first = [keep.tile([P, PACK, HALF_M], F32, name=f"w_first{h}", align_bytes=256) for h in range(2)]
+        w_second = keep.tile([P, PACK, M], F32, name="w_second", align_bytes=256)
+        ident = keep.tile([P, P], F32, name="ident", align_bytes=256)
+        neg_hi = keep.tile([P, PACK, M], F32, name="neg_hi", align_bytes=256)
+        lo_turned = keep.tile([P, M // P, 2, P, 2], BF16, name="lo_turned", align_bytes=256)
+        w_codes = [keep.tile([P, 2 * M], U32, name=f"w_codes{a}", align_bytes=256) for a in range(PASSES)]
+        w_scales = [keep.tile([P, 2 * M], U8, name=f"w_scales{a}", align_bytes=256) for a in range(PASSES)]
+        hi32 = keep.tile([P, PACK, M], F32, name="hi32", align_bytes=256)
+        picked_flat = [keep.tile([P, PACK * S + a * PIECE], F32, name=f"picked{a}", align_bytes=256) for a in range(PASSES)]
+        picked = [flat[:, 0 : PACK * S].rearrange("p (i j) -> p i j", i=PACK) for flat in picked_flat]
         x_first = picked_flat[1][:, PACK * S - PIECE :].bitcast(BF16).rearrange("p (j i) -> p j i", i=PACK)
         x_early = picked_flat[1][:, S : S + PIECE].bitcast(BF16).rearrange("p (j i) -> p j i", i=PACK)
         x_middle = picked_flat[1][:, 2 * S : 2 * S + PIECE].bitcast(BF16).rearrange("p (j i) -> p j i", i=PACK)
-        x_bf = [keep.tile([P, S, PACK], BF16, name=f"x_bf{a}", align_bytes=64) for a in range(PASSES)]
-        x_codes = [keep.tile([P, S], U32, name=f"x_codes{a}", align_bytes=64) for a in range(PASSES)]
-        x_scales = [keep.tile([P, S], U8, name=f"x_scales{a}", align_bytes=64) for a in range(PASSES)]
+        x_bf = [keep.tile([P, S, PACK], BF16, name=f"x_bf{a}", align_bytes=256) for a in range(PASSES)]
+        x_codes = [keep.tile([P, S], U32, name=f"x_codes{a}", align_bytes=256) for a in range(PASSES)]
+        x_scales = [keep.tile([P, S], U8, name=f"x_scales{a}", align_bytes=256) for a in range(PASSES)]
         acc = [psum.tile([P, M], F32, name=f"acc{j}") for j in range(S // P)]
-        result = [keep.tile([P, M], F32, name=f"result{j}") for j in range(S // P)]
+        result = [keep.tile([P, M], F32, name=f"result{j}", align_bytes=256) for j in range(S // P)]
 
         def by_runs(tile_view, axes):
             return tile_view.rearrange(axes + " -> p c i e", e=RUN)
@@ -193,8 +193,10 @@ def tile_list_heads_tm_hl_bias_kernel(tc, xT, w, wgt, b, offs, out):
             )
 
         def rounded(a, j0, c):
-            if j0 == 0:
-                return x_first if a == 1 else x_early
+            if a == 1 and j0 < PIECE:
+                return x_first[:, j0 : j0 + c, :]
+            if a == 0 and j0 == 0:
+                return x_early
             if a == 0 and j0 == HALF_S:
                 return x_middle
             return x_bf[a][:, j0 : j0 + c, :]
@@ -278,22 +280,22 @@ def tile_list_heads_tm_hl_bias_kernel(tc, xT, w, wgt, b, offs, out):
         gather(1, 1, 0, S)
         for j0, c in ((PIECE, PIECE), (HALF_S, P), (HALF_S + P, P)):
             multiply(0, j0, c)
-        round_pair(0, 0, P)
-        round_pair(0, P, HALF_S - P)
+        round_pair(0, 0, PIECE)
+        round_pair(0, PIECE, PIECE)
         gather(1, 2, 0, S)
         multiply(0, S - PIECE, PIECE)
 
         gather(1, 3, 0, PIECE)
-        round_pair(1, 0, P)
-        round_pair(1, P, P)
+        round_pair(1, 0, PIECE)
         gather(1, 3, PIECE, S - 2 * PIECE)
         multiply(1, 0, P)
+        multiply(1, P, P)
         gather(1, 3, S - PIECE, PIECE)
         round_pair(1, PIECE, PIECE)
         round_all(1, HALF_S, PIECE)
         round_all(1, S - 2 * P, P)
         round_all(1, S - P, P)
-        for j0, c in ((P, P), (PIECE, PIECE), (HALF_S, PIECE), (S - 2 * P, P), (S - P, P)):
+        for j0, c in ((PIECE, PIECE), (HALF_S, PIECE), (S - 2 * P, P), (S - P, P)):
             multiply(1, j0, c)
         last = S // P - 1
         for j in range(last):

@@ -28,6 +28,8 @@ HALF_M = M // 2
 PART = M * PACK
 WGT_ROW0 = P - 2 * GROUPS
 PIECE = 2 * P
+FIRST_LOADS = tuple((n0, n0 + P) for n0 in range(0, M, P))
+SECOND_LOADS = ((0, P), (P, M))
 PLANE_ORDER = ((0, 0), (0, 1), (0, 2), (1, 0), (0, 3), (1, 1), (1, 2), (1, 3))
 
 
@@ -48,24 +50,28 @@ def tile_list_heads_tm_hl_bias_kernel(tc, xT, w, wgt, b, offs, out):
         first_lo, first_hi, second_hi, second_lo = (
             room[:, part * PART : (part + 1) * PART].rearrange("p (n i) -> p n i", i=PACK) for part in range(4)
         )
-        turned_at = PART + PART // 2 - 2 * P
-        turned = room[:, turned_at : turned_at + 2 * S].bitcast(F32)
+        turned = room[:, PART + P : 2 * PART + P].bitcast(F32)
         bias = keep.tile([P, M], F32, name="bias", align_bytes=256)
         planes = [[keep.tile([P, T], F32, name=f"plane{a}{i}", align_bytes=256) for i in range(PACK)] for a in range(PASSES)]
-        w_first = [keep.tile([P, PACK, HALF_M], F32, name=f"w_first{h}", align_bytes=256) for h in range(2)]
-        w_second = keep.tile([P, PACK, M], F32, name="w_second", align_bytes=256)
+        w_first = {n0: keep.tile([P, PACK, n1 - n0], F32, name=f"w_first{n0}", align_bytes=256) for n0, n1 in FIRST_LOADS}
+        w_second = [keep.tile([P, PACK, n1 - n0], F32, name=f"w_second{n0}", align_bytes=256) for n0, n1 in SECOND_LOADS]
+        neg_first = keep.tile([P, PACK, P], F32, name="neg_first", align_bytes=256)
         ident = keep.tile([P, P], F32, name="ident", align_bytes=256)
-        neg_hi = keep.tile([P, PACK, M], F32, name="neg_hi", align_bytes=256)
-        lo_turned = keep.tile([P, M // P, 2, P, 2], BF16, name="lo_turned", align_bytes=256)
         w_codes = [keep.tile([P, 2 * M], U32, name=f"w_codes{a}", align_bytes=256) for a in range(PASSES)]
         w_scales = [keep.tile([P, 2 * M], U8, name=f"w_scales{a}", align_bytes=256) for a in range(PASSES)]
         hi32 = keep.tile([P, PACK, M], F32, name="hi32", align_bytes=256)
+        neg_hi = [neg_first[:], hi32[:, :, P:M]]
         picked_flat = [keep.tile([P, PACK * S + a * PIECE], F32, name=f"picked{a}", align_bytes=256) for a in range(PASSES)]
         picked = [flat[:, 0 : PACK * S].rearrange("p (i j) -> p i j", i=PACK) for flat in picked_flat]
         x_first = picked_flat[1][:, PACK * S - PIECE :].bitcast(BF16).rearrange("p (j i) -> p j i", i=PACK)
+        mask_columns = [
+            flat[:, at : at + 1].bitcast(I32)
+            for flat, at in ((picked_flat[1], 0), (picked_flat[0], 2 * S), (picked_flat[0], S))
+        ]
         x_early = picked_flat[1][:, S : S + PIECE].bitcast(BF16).rearrange("p (j i) -> p j i", i=PACK)
         x_middle = picked_flat[1][:, 2 * S : 2 * S + PIECE].bitcast(BF16).rearrange("p (j i) -> p j i", i=PACK)
         x_bf = [keep.tile([P, S, PACK], BF16, name=f"x_bf{a}", align_bytes=256) for a in range(PASSES)]
+        lo_words = x_bf[0][:, 0:HALF_S, :].rearrange("p j i -> p (j i)")
         x_codes = [keep.tile([P, S], U32, name=f"x_codes{a}", align_bytes=256) for a in range(PASSES)]
         x_scales = [keep.tile([P, S], U8, name=f"x_scales{a}", align_bytes=256) for a in range(PASSES)]
         acc = [psum.tile([P, M], F32, name=f"acc{j}") for j in range(S // P)]
@@ -104,49 +110,53 @@ def tile_list_heads_tm_hl_bias_kernel(tc, xT, w, wgt, b, offs, out):
             nc.scalar.copy(out=wgt_sb[:, h * HALF_S : (h + 1) * HALF_S], in_=acc[h][:])
 
 
-        def mask_first(h, n0):
-            at = h * HALF_M + n0
+        def w_block(at):
+            return w_first[at][:]
+
+        def mask_first(at):
             nc.vector.tensor_scalar(
                 out=hi32[:, :, at : at + P].bitcast(I32),
-                in0=w_first[h][:, :, n0 : n0 + P].bitcast(I32),
+                in0=w_block(at).bitcast(I32),
                 scalar1=HI_MASK,
                 scalar2=None,
                 op0=ALU.bitwise_and,
             )
 
-        def subtract_first(h, n0):
-            at = h * HALF_M + n0
+        def subtract_first(at):
             nc.vector.tensor_tensor(
                 out=interleaved(first_lo[:, at : at + P, :]),
-                in0=planar(w_first[h][:, :, n0 : n0 + P]),
+                in0=planar(w_block(at)),
                 in1=planar(hi32[:, :, at : at + P]),
                 op=ALU.subtract,
             )
 
-        def cast_first(h):
-            cols = slice(h * HALF_M, (h + 1) * HALF_M)
-            nc.scalar.copy(out=interleaved(first_hi[:, cols, :]), in_=planar(hi32[:, :, cols]))
+        def cast_first():
+            nc.scalar.copy(out=interleaved(first_hi), in_=planar(hi32[:]))
 
 
-        def mask_second():
+        def mask_second(nb):
+            h = min(nb, 1)
+            cols = slice((nb - h) * P, (nb - h + 1) * P)
             nc.vector.tensor_scalar(
-                out=neg_hi[:].bitcast(I32),
-                in0=w_second[:].bitcast(I32),
-                scalar1=HI_MASK,
+                out=neg_hi[h][:, :, cols].bitcast(I32),
+                in0=w_second[h][:, :, cols].bitcast(I32),
+                scalar1=mask_columns[nb - 1] if nb > 0 else HI_MASK,
                 scalar2=SIGN_BIT,
                 op0=ALU.bitwise_and,
                 op1=ALU.bitwise_xor,
             )
 
-        def cast_second():
-            nc.scalar.activation(out=interleaved(second_hi), in_=planar(neg_hi[:]), func=ACT.Copy, scale=-1.0)
+        def cast_second(h):
+            cols = slice(*SECOND_LOADS[h])
+            nc.scalar.activation(out=interleaved(second_hi[:, cols, :]), in_=planar(neg_hi[h]), func=ACT.Copy, scale=-1.0)
 
         def turn_lo(nb):
             bank = acc[(nb + 2) % 4]
-            cols = slice(nb * P, (nb + 1) * P)
+            h = min(nb, 1)
+            cols = slice((nb - h) * P, (nb - h + 1) * P)
             for i in range(PACK):
                 target = bank[:, i * P : (i + 1) * P]
-                for source, is_first in ((w_second, True), (neg_hi, False)):
+                for source, is_first in ((w_second[h], True), (neg_hi[h], False)):
                     nc.tensor.matmul(
                         target,
                         lhsT=source[:, i, cols],
@@ -156,16 +166,16 @@ def tile_list_heads_tm_hl_bias_kernel(tc, xT, w, wgt, b, offs, out):
                         is_transpose=True,
                     )
             nc.scalar.copy(
-                out=lo_turned[:, nb, :, :, :],
+                out=lo_words.rearrange("n (b u p e) -> n b u p e", u=2, p=P, e=2)[:, (nb + 2) % 4, :, :, :],
                 in_=bank[:].rearrange("n (u e p) -> n u p e", u=2, e=2),
             )
 
         def turn_lo_back(h):
             bank = acc[4 + h]
-            words = lo_turned[:].rearrange("n b u p e -> n (b u p e)").bitcast(F32)
+            words = lo_words.bitcast(F32)
             for u in range(2):
                 for block in range(2):
-                    at = ((2 * h + block) * 2 + u) * P
+                    at = ((2 * (1 - h) + block) * 2 + u) * P
                     to = (2 * u + block) * P
                     nc.tensor.transpose(bank[:, to : to + P], words[:, at : at + P], ident[:])
             nc.scalar.copy(
@@ -176,11 +186,11 @@ def tile_list_heads_tm_hl_bias_kernel(tc, xT, w, wgt, b, offs, out):
                 in_=bank[:].rearrange("p (u n) -> p n u", u=2),
             )
 
-        def quantize_w(a):
+        def quantize_w(a, at, c):
             nc.vector.quantize_mx(
-                out=w_codes[a][:].bitcast(FP8X4),
-                scales=w_scales[a][:],
-                in_=room[:, 2 * PART * a : 2 * PART * (a + 1)],
+                out=w_codes[a][:, at : at + c].bitcast(FP8X4),
+                scales=w_scales[a][:, at : at + c],
+                in_=room[:, 2 * PART * a + PACK * at : 2 * PART * a + PACK * (at + c)],
             )
 
 
@@ -234,12 +244,14 @@ def tile_list_heads_tm_hl_bias_kernel(tc, xT, w, wgt, b, offs, out):
 
         half_rows = wgt.rearrange("p (h c) -> (p h) c", h=2)
         nc.sync.dma_start(out=wgt_rows[WGT_ROW0:P, :], in_=half_rows[0 : 2 * P : 2 * GROUPS + 1, :])
-        for h in range(2):
-            nc.sync.dma_start(out=w_first[h][:], in_=w_view[0][:, :, h * HALF_M : (h + 1) * HALF_M])
+        for n0, n1 in FIRST_LOADS:
+            nc.sync.dma_start(out=w_first[n0][:], in_=w_view[0][:, :, n0:n1])
         nc.sync.dma_start(offsets[:], offs)
-        nc.sync.dma_start(out=w_second[:], in_=w_view[1])
-        for a, i in PLANE_ORDER:
+        nc.sync.dma_start(out=w_second[0][:], in_=w_view[1][:, :, 0:P])
+        for n, (a, i) in enumerate(PLANE_ORDER):
             nc.sync.dma_start(out=planes[a][i][:], in_=x_view[a, i])
+            if n == 0:
+                nc.sync.dma_start(out=w_second[1][:], in_=w_view[1][:, :, P:M])
         nc.sync.dma_start(out=bias[:], in_=b.partition_broadcast(P))
 
         nc.vector.memset(ident[:], 0.0)
@@ -249,27 +261,32 @@ def tile_list_heads_tm_hl_bias_kernel(tc, xT, w, wgt, b, offs, out):
             turn_wgt(v)
         for h in range(2):
             spread_wgt(h)
-        for h in range(2):
-            for n0 in (0, P):
-                mask_first(h, n0)
-            for n0 in (0, P):
-                subtract_first(h, n0)
-        for h in range(2):
-            cast_first(h)
+        for column in mask_columns:
+            nc.vector.memset(column, HI_MASK)
+        mask_first(0)
+        for at in range(0, M, P):
+            if at + P < M:
+                mask_first(at + P)
+            subtract_first(at)
+        mask_second(0)
+        quantize_w(0, 0, M)
         for h in range(2):
             fetch_wgt(h)
-        mask_second()
-        quantize_w(0)
-
-        gather(0, 0, 0, S)
+        cast_first()
+        gather(0, 0, 0, HALF_S)
+        gather(0, 0, HALF_S, HALF_S)
+        for nb in range(1, M // P):
+            mask_second(nb)
+        quantize_w(0, M, M)
         gather(0, 1, 0, S)
+        for h in range(2):
+            cast_second(h)
         for nb in range(M // P):
             turn_lo(nb)
         for h in range(2):
             turn_lo_back(h)
-        cast_second()
         gather(0, 2, 0, S)
-        quantize_w(1)
+        quantize_w(1, 0, 2 * M)
         gather(1, 0, 0, S)
         for j0 in (0, HALF_S):
             gather(0, 3, j0, HALF_S)

@@ -29,7 +29,6 @@ PART = M * PACK
 WGT_ROW0 = P - 2 * GROUPS
 PIECE = 2 * P
 FIRST_LOADS = tuple((n0, n0 + P) for n0 in range(0, M, P))
-SECOND_LOADS = ((0, P), (P, M))
 PLANE_ORDER = ((0, 0), (0, 1), (0, 2), (1, 0), (0, 3), (1, 1), (1, 2), (1, 3))
 
 
@@ -54,19 +53,19 @@ def tile_list_heads_tm_hl_bias_kernel(tc, xT, w, wgt, b, offs, out):
         bias = keep.tile([P, M], F32, name="bias", align_bytes=256)
         planes = [[keep.tile([P, T], F32, name=f"plane{a}{i}", align_bytes=256) for i in range(PACK)] for a in range(PASSES)]
         w_first = {n0: keep.tile([P, PACK, n1 - n0], F32, name=f"w_first{n0}", align_bytes=256) for n0, n1 in FIRST_LOADS}
-        w_second = [keep.tile([P, PACK, n1 - n0], F32, name=f"w_second{n0}", align_bytes=256) for n0, n1 in SECOND_LOADS]
-        neg_first = keep.tile([P, PACK, P], F32, name="neg_first", align_bytes=256)
+        w_second = [keep.tile([P, PACK, HALF_M], F32, name=f"w_second{h}", align_bytes=256) for h in range(2)]
         ident = keep.tile([P, P], F32, name="ident", align_bytes=256)
         w_codes = [keep.tile([P, 2 * M], U32, name=f"w_codes{a}", align_bytes=256) for a in range(PASSES)]
         w_scales = [keep.tile([P, 2 * M], U8, name=f"w_scales{a}", align_bytes=256) for a in range(PASSES)]
-        hi32 = keep.tile([P, PACK, M], F32, name="hi32", align_bytes=256)
-        neg_hi = [neg_first[:], hi32[:, :, P:M]]
+        hi_late = keep.tile([P, PACK, HALF_M], F32, name="hi_late", align_bytes=256)
         picked_flat = [keep.tile([P, PACK * S + a * PIECE], F32, name=f"picked{a}", align_bytes=256) for a in range(PASSES)]
         picked = [flat[:, 0 : PACK * S].rearrange("p (i j) -> p i j", i=PACK) for flat in picked_flat]
+        neg_hi = picked_flat[0][:, 3 * S : 4 * S].rearrange("p (i n) -> p i n", i=PACK)
+        hi32 = (neg_hi, hi_late[:])
         x_first = picked_flat[1][:, PACK * S - PIECE :].bitcast(BF16).rearrange("p (j i) -> p j i", i=PACK)
         mask_columns = [
             flat[:, at : at + 1].bitcast(I32)
-            for flat, at in ((picked_flat[1], 0), (picked_flat[0], 2 * S), (picked_flat[0], S))
+            for flat, at in ((picked_flat[0], S), (picked_flat[0], 2 * S), (picked_flat[1], 0))
         ]
         x_early = picked_flat[1][:, S : S + PIECE].bitcast(BF16).rearrange("p (j i) -> p j i", i=PACK)
         x_middle = picked_flat[1][:, 2 * S : 2 * S + PIECE].bitcast(BF16).rearrange("p (j i) -> p j i", i=PACK)
@@ -113,9 +112,12 @@ def tile_list_heads_tm_hl_bias_kernel(tc, xT, w, wgt, b, offs, out):
         def w_block(at):
             return w_first[at][:]
 
+        def hi_block(at):
+            return hi32[at // HALF_M][:, :, at % HALF_M : at % HALF_M + P]
+
         def mask_first(at):
             nc.vector.tensor_scalar(
-                out=hi32[:, :, at : at + P].bitcast(I32),
+                out=hi_block(at).bitcast(I32),
                 in0=w_block(at).bitcast(I32),
                 scalar1=HI_MASK,
                 scalar2=None,
@@ -126,43 +128,42 @@ def tile_list_heads_tm_hl_bias_kernel(tc, xT, w, wgt, b, offs, out):
             nc.vector.tensor_tensor(
                 out=interleaved(first_lo[:, at : at + P, :]),
                 in0=planar(w_block(at)),
-                in1=planar(hi32[:, :, at : at + P]),
+                in1=planar(hi_block(at)),
                 op=ALU.subtract,
             )
 
-        def cast_first():
-            nc.scalar.copy(out=interleaved(first_hi), in_=planar(hi32[:]))
+        def cast_first(h):
+            cols = slice(h * HALF_M, (h + 1) * HALF_M)
+            nc.scalar.copy(out=interleaved(first_hi[:, cols, :]), in_=planar(hi32[h]))
 
 
         def mask_second(nb):
-            h = min(nb, 1)
-            cols = slice((nb - h) * P, (nb - h + 1) * P)
+            h = nb // 2
+            cols = slice(nb % 2 * P, (nb % 2 + 1) * P)
             nc.vector.tensor_scalar(
-                out=neg_hi[h][:, :, cols].bitcast(I32),
+                out=neg_hi[:, :, cols].bitcast(I32),
                 in0=w_second[h][:, :, cols].bitcast(I32),
-                scalar1=mask_columns[nb - 1] if nb > 0 else HI_MASK,
+                scalar1=mask_columns[nb] if nb < 3 else HI_MASK,
                 scalar2=SIGN_BIT,
                 op0=ALU.bitwise_and,
                 op1=ALU.bitwise_xor,
             )
 
         def cast_second(h):
-            cols = slice(*SECOND_LOADS[h])
-            nc.scalar.activation(out=interleaved(second_hi[:, cols, :]), in_=planar(neg_hi[h]), func=ACT.Copy, scale=-1.0)
+            cols = slice(h * HALF_M, (h + 1) * HALF_M)
+            nc.scalar.activation(out=interleaved(second_hi[:, cols, :]), in_=planar(neg_hi), func=ACT.Copy, scale=-1.0)
 
         def turn_lo(nb):
             bank = acc[(nb + 2) % 4]
-            h = min(nb, 1)
-            cols = slice((nb - h) * P, (nb - h + 1) * P)
-            for i in range(PACK):
-                target = bank[:, i * P : (i + 1) * P]
-                for source, is_first in ((w_second[h], True), (neg_hi[h], False)):
+            cols = slice(nb % 2 * P, (nb % 2 + 1) * P)
+            for n, source in enumerate((w_second[nb // 2], neg_hi)):
+                for i in range(PACK):
                     nc.tensor.matmul(
-                        target,
+                        bank[:, i * P : (i + 1) * P],
                         lhsT=source[:, i, cols],
                         rhs=ident[:],
-                        start=is_first,
-                        stop=not is_first,
+                        start=(n == 0 and i == 0),
+                        stop=(n == 1 and i == PACK - 1),
                         is_transpose=True,
                     )
             nc.scalar.copy(
@@ -247,11 +248,10 @@ def tile_list_heads_tm_hl_bias_kernel(tc, xT, w, wgt, b, offs, out):
         for n0, n1 in FIRST_LOADS:
             nc.sync.dma_start(out=w_first[n0][:], in_=w_view[0][:, :, n0:n1])
         nc.sync.dma_start(offsets[:], offs)
-        nc.sync.dma_start(out=w_second[0][:], in_=w_view[1][:, :, 0:P])
         for n, (a, i) in enumerate(PLANE_ORDER):
             nc.sync.dma_start(out=planes[a][i][:], in_=x_view[a, i])
-            if n == 0:
-                nc.sync.dma_start(out=w_second[1][:], in_=w_view[1][:, :, P:M])
+            if n in (0, 2):
+                nc.sync.dma_start(out=w_second[n // 2][:], in_=w_view[1][:, :, n // 2 * HALF_M : (n // 2 + 1) * HALF_M])
         nc.sync.dma_start(out=bias[:], in_=b.partition_broadcast(P))
 
         nc.vector.memset(ident[:], 0.0)
@@ -268,25 +268,25 @@ def tile_list_heads_tm_hl_bias_kernel(tc, xT, w, wgt, b, offs, out):
             if at + P < M:
                 mask_first(at + P)
             subtract_first(at)
-        mask_second(0)
         quantize_w(0, 0, M)
         for h in range(2):
             fetch_wgt(h)
-        cast_first()
+        for h in range(2):
+            cast_first(h)
         gather(0, 0, 0, HALF_S)
         gather(0, 0, HALF_S, HALF_S)
-        for nb in range(1, M // P):
-            mask_second(nb)
-        quantize_w(0, M, M)
-        gather(0, 1, 0, S)
         for h in range(2):
+            for nb in (2 * h, 2 * h + 1):
+                mask_second(nb)
+            if h == 0:
+                quantize_w(0, M, M)
             cast_second(h)
-        for nb in range(M // P):
-            turn_lo(nb)
-        for h in range(2):
+            for nb in (2 * h, 2 * h + 1):
+                turn_lo(nb)
             turn_lo_back(h)
-        gather(0, 2, 0, S)
-        quantize_w(1, 0, 2 * M)
+            if h == 0:
+                gather(0, 1, 0, S)
+                gather(0, 2, 0, S)
         gather(1, 0, 0, S)
         for j0 in (0, HALF_S):
             gather(0, 3, j0, HALF_S)
@@ -295,6 +295,7 @@ def tile_list_heads_tm_hl_bias_kernel(tc, xT, w, wgt, b, offs, out):
         multiply(0, 0, P)
         multiply(0, P, P)
         gather(1, 1, 0, S)
+        quantize_w(1, 0, 2 * M)
         for j0, c in ((PIECE, PIECE), (HALF_S, P), (HALF_S + P, P)):
             multiply(0, j0, c)
         round_pair(0, 0, PIECE)

@@ -29,7 +29,7 @@ PART = M * PACK
 WGT_ROW0 = P - 2 * GROUPS
 PIECE = 2 * P
 FIRST_LOADS = tuple((n0, n0 + P) for n0 in range(0, M, P))
-PLANE_ORDER = ((0, 0), (0, 1), (0, 2), (1, 0), (0, 3), (1, 1), (1, 2), (1, 3))
+PLANE_ORDER = tuple((a, i) for a in range(PASSES) for i in range(PACK))
 
 
 def tile_list_heads_tm_hl_bias_kernel(tc, xT, w, wgt, b, offs, out):
@@ -45,11 +45,11 @@ def tile_list_heads_tm_hl_bias_kernel(tc, xT, w, wgt, b, offs, out):
         offsets = lists.tile([P, S // PER_OFFSET_COLUMN], U16, name="offsets")
         wgt_sb = keep.tile([P, S], F32, name="wgt_sb", align_bytes=256)
         wgt_rows = keep.tile([P, HALF_S], F32, name="wgt_rows", align_bytes=256)
-        room = keep.tile([P, 4 * PART], BF16, name="room", align_bytes=256)
-        first_lo, first_hi, second_hi, second_lo = (
-            room[:, part * PART : (part + 1) * PART].rearrange("p (n i) -> p n i", i=PACK) for part in range(4)
+        room = keep.tile([P, 2 * PART], BF16, name="room", align_bytes=256)
+        first_lo, first_hi = (
+            room[:, part * PART : (part + 1) * PART].rearrange("p (n i) -> p n i", i=PACK) for part in range(2)
         )
-        turned = room[:, PART + P : 2 * PART + P].bitcast(F32)
+        turned = room[:, PART : 2 * PART].bitcast(F32)
         bias = keep.tile([P, M], F32, name="bias", align_bytes=256)
         planes = [[keep.tile([P, T], F32, name=f"plane{a}{i}", align_bytes=256) for i in range(PACK)] for a in range(PASSES)]
         w_first = {n0: keep.tile([P, PACK, n1 - n0], F32, name=f"w_first{n0}", align_bytes=256) for n0, n1 in FIRST_LOADS}
@@ -57,20 +57,30 @@ def tile_list_heads_tm_hl_bias_kernel(tc, xT, w, wgt, b, offs, out):
         ident = keep.tile([P, P], F32, name="ident", align_bytes=256)
         w_codes = [keep.tile([P, 2 * M], U32, name=f"w_codes{a}", align_bytes=256) for a in range(PASSES)]
         w_scales = [keep.tile([P, 2 * M], U8, name=f"w_scales{a}", align_bytes=256) for a in range(PASSES)]
-        hi_late = keep.tile([P, PACK, HALF_M], F32, name="hi_late", align_bytes=256)
-        picked_flat = [keep.tile([P, PACK * S + a * PIECE], F32, name=f"picked{a}", align_bytes=256) for a in range(PASSES)]
+        early_hi = keep.tile([P, HALF_S], F32, name="early_hi", align_bytes=256)
+        late_lo = keep.tile([P, HALF_S], F32, name="late_lo", align_bytes=256)
+        picked_flat = [keep.tile([P, PACK * S + a * S], F32, name=f"picked{a}", align_bytes=256) for a in range(PASSES)]
         picked = [flat[:, 0 : PACK * S].rearrange("p (i j) -> p i j", i=PACK) for flat in picked_flat]
-        neg_hi = picked_flat[0][:, 3 * S : 4 * S].rearrange("p (i n) -> p i n", i=PACK)
-        hi32 = (neg_hi, hi_late[:])
-        x_first = picked_flat[1][:, PACK * S - PIECE :].bitcast(BF16).rearrange("p (j i) -> p j i", i=PACK)
-        mask_columns = [
-            flat[:, at : at + 1].bitcast(I32)
-            for flat, at in ((picked_flat[0], S), (picked_flat[0], 2 * S), (picked_flat[1], 0))
-        ]
-        x_early = picked_flat[1][:, S : S + PIECE].bitcast(BF16).rearrange("p (j i) -> p j i", i=PACK)
-        x_middle = picked_flat[1][:, 2 * S : 2 * S + PIECE].bitcast(BF16).rearrange("p (j i) -> p j i", i=PACK)
-        x_bf = [keep.tile([P, S, PACK], BF16, name=f"x_bf{a}", align_bytes=256) for a in range(PASSES)]
-        lo_words = x_bf[0][:, 0:HALF_S, :].rearrange("p j i -> p (j i)")
+
+        def lodged(a, at):
+            return picked_flat[a][:, at : at + HALF_S].bitcast(BF16)
+
+        hi32 = picked_flat[1][:, 3 * HALF_S : 7 * HALF_S].rearrange("p (i n) -> p i n", i=PACK)
+        neg_hi = picked_flat[1][:, 5 * HALF_S : 7 * HALF_S].rearrange("p (i n) -> p i n", i=PACK)
+        second_hi = (early_hi[:].bitcast(BF16), lodged(0, 0))
+        second_lo = (lodged(1, 0), late_lo[:].bitcast(BF16))
+        early_words = lodged(1, S + PIECE - 7 * P // 2)
+        lo_words = (
+            early_words[:, 0:HALF_S],
+            early_words[:, HALF_S:S],
+            lodged(0, S)[:, 0:HALF_S],
+            lodged(1, PACK * S)[:, 0:HALF_S] ,
+        )
+        first_places = tuple(PIECE * at for at in (3, 4, 5, 8, 11, 12, 14, 17))
+        x_first = lodged(1, PACK * S - PIECE)
+        mask_column = picked_flat[0][:, 2 * S : 2 * S + 1].bitcast(I32)
+        x_second = lodged(0, 3 * S - PIECE)
+        x_late = keep.tile([P, HALF_S, PACK], BF16, name="x_late", align_bytes=256)
         x_codes = [keep.tile([P, S], U32, name=f"x_codes{a}", align_bytes=256) for a in range(PASSES)]
         x_scales = [keep.tile([P, S], U8, name=f"x_scales{a}", align_bytes=256) for a in range(PASSES)]
         acc = [psum.tile([P, M], F32, name=f"acc{j}") for j in range(S // P)]
@@ -87,12 +97,12 @@ def tile_list_heads_tm_hl_bias_kernel(tc, xT, w, wgt, b, offs, out):
 
 
         def turn_wgt(v):
-            bank = acc[2 + v]
+            bank = acc[v]
             for u in range(2):
                 at = (2 * v + u) * P
                 nc.tensor.transpose(bank[:, u * P : (u + 1) * P], wgt_rows[:, at : at + P], ident[:])
             nc.scalar.copy(
-                out=turned.rearrange("j (h u g r) -> j h u g r", h=2, u=4, g=GROUPS)[:, :, 2 * v : 2 * v + 2, :, :],
+                out=turned.rearrange("j (u h g r) -> j h u g r", h=2, u=4, g=GROUPS)[:, :, 2 * v : 2 * v + 2, :, :],
                 in_=bank[:, 0 : 2 * P]
                 .rearrange("j (u q) -> j u q", u=2)[:, :, WGT_ROW0:]
                 .rearrange("j u (g h) -> j h u g", h=2)
@@ -102,18 +112,18 @@ def tile_list_heads_tm_hl_bias_kernel(tc, xT, w, wgt, b, offs, out):
 
         def spread_wgt(h):
             for block in range(HALF_S // P):
-                at = h * HALF_S + block * P
-                nc.tensor.transpose(acc[h][:, block * P : (block + 1) * P], turned[:, at : at + P], ident[:])
+                at = (2 * block + h) * P
+                nc.tensor.transpose(acc[6 + h][:, block * P : (block + 1) * P], turned[:, at : at + P], ident[:])
 
         def fetch_wgt(h):
-            nc.scalar.copy(out=wgt_sb[:, h * HALF_S : (h + 1) * HALF_S], in_=acc[h][:])
+            nc.scalar.copy(out=wgt_sb[:, h * HALF_S : (h + 1) * HALF_S], in_=acc[6 + h][:])
 
 
         def w_block(at):
             return w_first[at][:]
 
         def hi_block(at):
-            return hi32[at // HALF_M][:, :, at % HALF_M : at % HALF_M + P]
+            return hi32[:, :, at : at + P]
 
         def mask_first(at):
             nc.vector.tensor_scalar(
@@ -132,9 +142,8 @@ def tile_list_heads_tm_hl_bias_kernel(tc, xT, w, wgt, b, offs, out):
                 op=ALU.subtract,
             )
 
-        def cast_first(h):
-            cols = slice(h * HALF_M, (h + 1) * HALF_M)
-            nc.scalar.copy(out=interleaved(first_hi[:, cols, :]), in_=planar(hi32[h]))
+        def cast_first(at):
+            nc.scalar.copy(out=interleaved(first_hi[:, at : at + P, :]), in_=planar(hi_block(at)))
 
 
         def mask_second(nb):
@@ -143,18 +152,18 @@ def tile_list_heads_tm_hl_bias_kernel(tc, xT, w, wgt, b, offs, out):
             nc.vector.tensor_scalar(
                 out=neg_hi[:, :, cols].bitcast(I32),
                 in0=w_second[h][:, :, cols].bitcast(I32),
-                scalar1=mask_columns[nb] if nb < 3 else HI_MASK,
+                scalar1=mask_column if nb == 1 else HI_MASK,
                 scalar2=SIGN_BIT,
                 op0=ALU.bitwise_and,
                 op1=ALU.bitwise_xor,
             )
 
         def cast_second(h):
-            cols = slice(h * HALF_M, (h + 1) * HALF_M)
-            nc.scalar.activation(out=interleaved(second_hi[:, cols, :]), in_=planar(neg_hi), func=ACT.Copy, scale=-1.0)
+            target = second_hi[h].rearrange("p (n i) -> p n i", i=PACK)
+            nc.scalar.activation(out=interleaved(target), in_=planar(neg_hi), func=ACT.Copy, scale=-1.0)
 
         def turn_lo(nb):
-            bank = acc[(nb + 2) % 4]
+            bank = acc[(6, 7, 7, 6)[nb]]
             cols = slice(nb % 2 * P, (nb % 2 + 1) * P)
             for n, source in enumerate((w_second[nb // 2], neg_hi)):
                 for i in range(PACK):
@@ -167,31 +176,28 @@ def tile_list_heads_tm_hl_bias_kernel(tc, xT, w, wgt, b, offs, out):
                         is_transpose=True,
                     )
             nc.scalar.copy(
-                out=lo_words.rearrange("n (b u p e) -> n b u p e", u=2, p=P, e=2)[:, (nb + 2) % 4, :, :, :],
+                out=lo_words[nb].rearrange("n (u p e) -> n u p e", u=2, e=2),
                 in_=bank[:].rearrange("n (u e p) -> n u p e", u=2, e=2),
             )
 
         def turn_lo_back(h):
-            bank = acc[4 + h]
-            words = lo_words.bitcast(F32)
+            bank = acc[6 + h]
             for u in range(2):
                 for block in range(2):
-                    at = ((2 * (1 - h) + block) * 2 + u) * P
+                    words = lo_words[2 * h + block].bitcast(F32)[:, u * P : (u + 1) * P]
                     to = (2 * u + block) * P
-                    nc.tensor.transpose(bank[:, to : to + P], words[:, at : at + P], ident[:])
+                    nc.tensor.transpose(bank[:, to : to + P], words, ident[:])
             nc.scalar.copy(
-                out=second_lo[:, h * HALF_M : (h + 1) * HALF_M, :]
-                .rearrange("p n i -> p (n i)")
-                .bitcast(F32)
-                .rearrange("p (n u) -> p n u", u=2),
+                out=second_lo[h].bitcast(F32).rearrange("p (n u) -> p n u", u=2),
                 in_=bank[:].rearrange("p (u n) -> p n u", u=2),
             )
 
-        def quantize_w(a, at, c):
+        def quantize_w(a, at, values):
+            c = values.shape[1] // PACK
             nc.vector.quantize_mx(
                 out=w_codes[a][:, at : at + c].bitcast(FP8X4),
                 scales=w_scales[a][:, at : at + c],
-                in_=room[:, 2 * PART * a + PACK * at : 2 * PART * a + PACK * (at + c)],
+                in_=values,
             )
 
 
@@ -204,16 +210,24 @@ def tile_list_heads_tm_hl_bias_kernel(tc, xT, w, wgt, b, offs, out):
             )
 
         def rounded(a, j0, c):
-            if a == 1 and j0 < PIECE:
-                return x_first[:, j0 : j0 + c, :]
-            if a == 0 and j0 == 0:
-                return x_early
-            if a == 0 and j0 == HALF_S:
-                return x_middle
-            return x_bf[a][:, j0 : j0 + c, :]
+            if a == 1 and j0 >= HALF_S:
+                return x_late[:, j0 - HALF_S : j0 - HALF_S + c, :]
+            if a == 0:
+                at = first_places[j0 // P]
+                return picked_flat[1][:, at : at + 2 * c].bitcast(BF16).rearrange("p (j i) -> p j i", i=PACK)
+            piece = (x_first, x_second)[j0 // PIECE]
+            return piece.rearrange("p (j i) -> p j i", i=PACK)[:, j0 % PIECE : j0 % PIECE + c, :]
 
         def round_all(a, j0, c):
             nc.scalar.copy(out=interleaved(rounded(a, j0, c)), in_=planar(picked[a][:, :, j0 : j0 + c]))
+
+        def round_first(j0):
+            at, then = first_places[j0 // P : j0 // P + 2]
+            both = picked_flat[1][:, at : 2 * then - at].bitcast(BF16).rearrange("p (b r) -> p b r", b=2)
+            nc.scalar.copy(
+                out=both[:, :, 0 : PACK * P].rearrange("p b (c e i) -> p b c i e", e=RUN, i=PACK),
+                in_=picked[0][:, :, j0 : j0 + PIECE].rearrange("p i (b c e) -> p b c i e", b=2, e=RUN),
+            )
 
         def round_pair(u, j0, c):
             pair = slice(2 * u, 2 * u + 2)
@@ -250,7 +264,7 @@ def tile_list_heads_tm_hl_bias_kernel(tc, xT, w, wgt, b, offs, out):
         nc.sync.dma_start(offsets[:], offs)
         for n, (a, i) in enumerate(PLANE_ORDER):
             nc.sync.dma_start(out=planes[a][i][:], in_=x_view[a, i])
-            if n in (0, 2):
+            if n in (1, 3):
                 nc.sync.dma_start(out=w_second[n // 2][:], in_=w_view[1][:, :, n // 2 * HALF_M : (n // 2 + 1) * HALF_M])
         nc.sync.dma_start(out=bias[:], in_=b.partition_broadcast(P))
 
@@ -261,50 +275,64 @@ def tile_list_heads_tm_hl_bias_kernel(tc, xT, w, wgt, b, offs, out):
             turn_wgt(v)
         for h in range(2):
             spread_wgt(h)
-        for column in mask_columns:
-            nc.vector.memset(column, HI_MASK)
+        nc.vector.memset(mask_column, HI_MASK)
         mask_first(0)
         for at in range(0, M, P):
             if at + P < M:
                 mask_first(at + P)
             subtract_first(at)
-        quantize_w(0, 0, M)
+        quantize_w(0, 0, room[:, 0:PART])
         for h in range(2):
             fetch_wgt(h)
-        for h in range(2):
-            cast_first(h)
+        for at in range(0, M, P):
+            cast_first(at)
         gather(0, 0, 0, HALF_S)
         gather(0, 0, HALF_S, HALF_S)
-        for h in range(2):
-            for nb in (2 * h, 2 * h + 1):
-                mask_second(nb)
-            if h == 0:
-                quantize_w(0, M, M)
+        gather(0, 1, 0, S)
+
+        def split_second(h):
             cast_second(h)
             for nb in (2 * h, 2 * h + 1):
                 turn_lo(nb)
             turn_lo_back(h)
-            if h == 0:
-                gather(0, 1, 0, S)
-                gather(0, 2, 0, S)
-        gather(1, 0, 0, S)
+
+        def quantize_second(h):
+            quantize_w(1, h * HALF_M, second_hi[h])
+            quantize_w(1, M + h * HALF_M, second_lo[h])
+
+        mask_second(0)
+        mask_second(1)
+        quantize_w(0, M, room[:, PART : 2 * PART])
+        split_second(0)
+        gather(0, 2, 0, S)
         for j0 in (0, HALF_S):
             gather(0, 3, j0, HALF_S)
-        for j0, c in ((0, P), (P, P), (PIECE, PIECE), (HALF_S, P), (HALF_S + P, P), (S - PIECE, PIECE)):
-            round_all(0, j0, c)
+        mask_second(2)
+        mask_second(3)
+        quantize_second(0)
+        round_first(0)
+        round_first(PIECE)
+        split_second(1)
+        round_first(HALF_S)
+        round_first(S - PIECE)
         multiply(0, 0, P)
         multiply(0, P, P)
+        gather(1, 0, 0, S)
+        multiply(0, 2 * P, P)
+        multiply(0, 3 * P, P)
         gather(1, 1, 0, S)
-        quantize_w(1, 0, 2 * M)
-        for j0, c in ((PIECE, PIECE), (HALF_S, P), (HALF_S + P, P)):
-            multiply(0, j0, c)
-        round_pair(0, 0, PIECE)
-        round_pair(0, PIECE, PIECE)
+        quantize_w(1, HALF_M, second_hi[1])
+        multiply(0, 4 * P, P)
+        multiply(0, 5 * P, P)
         gather(1, 2, 0, S)
-        multiply(0, S - PIECE, PIECE)
+        quantize_w(1, M + HALF_M, second_lo[1])
 
         gather(1, 3, 0, PIECE)
+        round_pair(0, 0, PIECE)
+        round_pair(0, PIECE, PIECE)
         round_pair(1, 0, PIECE)
+        multiply(0, 6 * P, P)
+        multiply(0, 7 * P, P)
         gather(1, 3, PIECE, S - 2 * PIECE)
         multiply(1, 0, P)
         multiply(1, P, P)

@@ -58,28 +58,31 @@ def tile_list_heads_tm_hl_bias_kernel(tc, xT, w, wgt, b, offs, out):
         w_codes = [keep.tile([P, 2 * M], U32, name=f"w_codes{a}", align_bytes=256) for a in range(PASSES)]
         w_scales = [keep.tile([P, 2 * M], U8, name=f"w_scales{a}", align_bytes=256) for a in range(PASSES)]
         early_hi = keep.tile([P, HALF_S], F32, name="early_hi", align_bytes=256)
-        late_lo = keep.tile([P, HALF_S], F32, name="late_lo", align_bytes=256)
-        picked_flat = [keep.tile([P, PACK * S + a * S], F32, name=f"picked{a}", align_bytes=256) for a in range(PASSES)]
-        picked = [flat[:, 0 : PACK * S].rearrange("p (i j) -> p i j", i=PACK) for flat in picked_flat]
+        lo_tiles = [keep.tile([P, HALF_S], F32, name=f"second_lo{h}", align_bytes=256) for h in range(2)]
+        picked_flat = [keep.tile([P, PACK * S + PIECE], F32, name=f"picked{a}", align_bytes=256) for a in range(PASSES)]
+        picked = [
+            flat[:, at : at + PACK * S].rearrange("p (i j) -> p i j", i=PACK)
+            for flat, at in zip(picked_flat, (PIECE, 0))
+        ]
 
         def lodged(a, at):
             return picked_flat[a][:, at : at + HALF_S].bitcast(BF16)
 
-        hi32 = picked_flat[1][:, 3 * HALF_S : 7 * HALF_S].rearrange("p (i n) -> p i n", i=PACK)
-        neg_hi = picked_flat[1][:, 5 * HALF_S : 7 * HALF_S].rearrange("p (i n) -> p i n", i=PACK)
+        hi32 = picked_flat[1][:, 5 * PIECE : 13 * PIECE].rearrange("p (i n) -> p i n", i=PACK)
+        neg_hi = picked_flat[1][:, 9 * PIECE : 13 * PIECE].rearrange("p (i n) -> p i n", i=PACK)
         second_hi = (early_hi[:].bitcast(BF16), lodged(0, 0))
-        second_lo = (lodged(1, 0), late_lo[:].bitcast(BF16))
-        early_words = lodged(1, S + PIECE - 7 * P // 2)
+        second_lo = [tile[:].bitcast(BF16) for tile in lo_tiles]
+        early_words = lodged(1, 7 * PIECE)
         lo_words = (
             early_words[:, 0:HALF_S],
             early_words[:, HALF_S:S],
-            lodged(0, S)[:, 0:HALF_S],
-            lodged(1, PACK * S)[:, 0:HALF_S] ,
+            lodged(0, PIECE + S)[:, 0:HALF_S],
+            lodged(1, 15 * PIECE - P)[:, 0:HALF_S],
         )
-        first_places = tuple(PIECE * at for at in (3, 4, 5, 8, 11, 12, 14, 17))
+        first_places = tuple(PIECE * at for at in (7, 8, 9, 10, 11, 13, 12, 14))
         x_first = lodged(1, PACK * S - PIECE)
-        mask_column = picked_flat[0][:, 2 * S : 2 * S + 1].bitcast(I32)
-        x_second = lodged(0, 3 * S - PIECE)
+        mask_columns = [flat[:, at : at + 1].bitcast(I32) for flat, at in ((picked_flat[0], PIECE + 2 * S), (picked_flat[1], 0))]
+        x_second = lodged(0, 3 * S)
         x_late = keep.tile([P, HALF_S, PACK], BF16, name="x_late", align_bytes=256)
         x_codes = [keep.tile([P, S], U32, name=f"x_codes{a}", align_bytes=256) for a in range(PASSES)]
         x_scales = [keep.tile([P, S], U8, name=f"x_scales{a}", align_bytes=256) for a in range(PASSES)]
@@ -97,7 +100,7 @@ def tile_list_heads_tm_hl_bias_kernel(tc, xT, w, wgt, b, offs, out):
 
 
         def turn_wgt(v):
-            bank = acc[v]
+            bank = acc[2 + v]
             for u in range(2):
                 at = (2 * v + u) * P
                 nc.tensor.transpose(bank[:, u * P : (u + 1) * P], wgt_rows[:, at : at + P], ident[:])
@@ -113,46 +116,41 @@ def tile_list_heads_tm_hl_bias_kernel(tc, xT, w, wgt, b, offs, out):
         def spread_wgt(h):
             for block in range(HALF_S // P):
                 at = (2 * block + h) * P
-                nc.tensor.transpose(acc[6 + h][:, block * P : (block + 1) * P], turned[:, at : at + P], ident[:])
+                nc.tensor.transpose(acc[h][:, block * P : (block + 1) * P], turned[:, at : at + P], ident[:])
 
         def fetch_wgt(h):
-            nc.scalar.copy(out=wgt_sb[:, h * HALF_S : (h + 1) * HALF_S], in_=acc[6 + h][:])
+            nc.scalar.copy(out=wgt_sb[:, h * HALF_S : (h + 1) * HALF_S], in_=acc[h][:])
 
 
-        def w_block(at):
-            return w_first[at][:]
+        def w_block(at, c):
+            return w_first[at // P * P][:, :, at % P : at % P + c]
 
-        def hi_block(at):
-            return hi32[:, :, at : at + P]
-
-        def mask_first(at):
+        def mask_first(at, c):
             nc.vector.tensor_scalar(
-                out=hi_block(at).bitcast(I32),
-                in0=w_block(at).bitcast(I32),
+                out=hi32[:, :, at : at + c].bitcast(I32),
+                in0=w_block(at, c).bitcast(I32),
                 scalar1=HI_MASK,
                 scalar2=None,
                 op0=ALU.bitwise_and,
             )
 
-        def subtract_first(at):
+        def subtract_first(at, c):
             nc.vector.tensor_tensor(
-                out=interleaved(first_lo[:, at : at + P, :]),
-                in0=planar(w_block(at)),
-                in1=planar(hi_block(at)),
+                out=interleaved(first_lo[:, at : at + c, :]),
+                in0=planar(w_block(at, c)),
+                in1=planar(hi32[:, :, at : at + c]),
                 op=ALU.subtract,
             )
 
         def cast_first(at):
-            nc.scalar.copy(out=interleaved(first_hi[:, at : at + P, :]), in_=planar(hi_block(at)))
+            nc.scalar.copy(out=interleaved(first_hi[:, at : at + P, :]), in_=planar(hi32[:, :, at : at + P]))
 
 
-        def mask_second(nb):
-            h = nb // 2
-            cols = slice(nb % 2 * P, (nb % 2 + 1) * P)
+        def mask_second(h):
             nc.vector.tensor_scalar(
-                out=neg_hi[:, :, cols].bitcast(I32),
-                in0=w_second[h][:, :, cols].bitcast(I32),
-                scalar1=mask_column if nb == 1 else HI_MASK,
+                out=neg_hi.bitcast(I32),
+                in0=w_second[h][:].bitcast(I32),
+                scalar1=mask_columns[h],
                 scalar2=SIGN_BIT,
                 op0=ALU.bitwise_and,
                 op1=ALU.bitwise_xor,
@@ -163,7 +161,7 @@ def tile_list_heads_tm_hl_bias_kernel(tc, xT, w, wgt, b, offs, out):
             nc.scalar.activation(out=interleaved(target), in_=planar(neg_hi), func=ACT.Copy, scale=-1.0)
 
         def turn_lo(nb):
-            bank = acc[(6, 7, 7, 6)[nb]]
+            bank = acc[(0, 1, 1, 0)[nb]]
             cols = slice(nb % 2 * P, (nb % 2 + 1) * P)
             for n, source in enumerate((w_second[nb // 2], neg_hi)):
                 for i in range(PACK):
@@ -181,7 +179,7 @@ def tile_list_heads_tm_hl_bias_kernel(tc, xT, w, wgt, b, offs, out):
             )
 
         def turn_lo_back(h):
-            bank = acc[6 + h]
+            bank = acc[h]
             for u in range(2):
                 for block in range(2):
                     words = lo_words[2 * h + block].bitcast(F32)[:, u * P : (u + 1) * P]
@@ -275,13 +273,14 @@ def tile_list_heads_tm_hl_bias_kernel(tc, xT, w, wgt, b, offs, out):
             turn_wgt(v)
         for h in range(2):
             spread_wgt(h)
-        nc.vector.memset(mask_column, HI_MASK)
-        mask_first(0)
-        for at in range(0, M, P):
-            if at + P < M:
-                mask_first(at + P)
-            subtract_first(at)
-        quantize_w(0, 0, room[:, 0:PART])
+        for column in mask_columns:
+            nc.vector.memset(column, HI_MASK)
+        for at, c in ((0, P // 2), (P, P // 2), (2 * P, P)):
+            for step in (mask_first, subtract_first):
+                step(at, c)
+                step(at + c, c)
+        quantize_w(0, 0, room[:, 0 : PART - PACK * P])
+        quantize_w(0, M - P, room[:, PART - PACK * P : PART])
         for h in range(2):
             fetch_wgt(h)
         for at in range(0, M, P):
@@ -296,43 +295,37 @@ def tile_list_heads_tm_hl_bias_kernel(tc, xT, w, wgt, b, offs, out):
                 turn_lo(nb)
             turn_lo_back(h)
 
-        def quantize_second(h):
-            quantize_w(1, h * HALF_M, second_hi[h])
-            quantize_w(1, M + h * HALF_M, second_lo[h])
-
         mask_second(0)
-        mask_second(1)
         quantize_w(0, M, room[:, PART : 2 * PART])
         split_second(0)
         gather(0, 2, 0, S)
         for j0 in (0, HALF_S):
             gather(0, 3, j0, HALF_S)
-        mask_second(2)
-        mask_second(3)
-        quantize_second(0)
+        mask_second(1)
+        quantize_w(1, 0, second_hi[0])
+        gather(1, 0, 0, S)
+        quantize_w(1, M, second_lo[0])
         round_first(0)
-        round_first(PIECE)
         split_second(1)
+        round_first(PIECE)
         round_first(HALF_S)
         round_first(S - PIECE)
         multiply(0, 0, P)
         multiply(0, P, P)
-        gather(1, 0, 0, S)
-        multiply(0, 2 * P, P)
-        multiply(0, 3 * P, P)
         gather(1, 1, 0, S)
+        multiply(0, PIECE, PIECE)
         quantize_w(1, HALF_M, second_hi[1])
         multiply(0, 4 * P, P)
         multiply(0, 5 * P, P)
         gather(1, 2, 0, S)
         quantize_w(1, M + HALF_M, second_lo[1])
+        multiply(0, 6 * P, P)
+        multiply(0, 7 * P, P)
 
         gather(1, 3, 0, PIECE)
         round_pair(0, 0, PIECE)
         round_pair(0, PIECE, PIECE)
         round_pair(1, 0, PIECE)
-        multiply(0, 6 * P, P)
-        multiply(0, 7 * P, P)
         gather(1, 3, PIECE, S - 2 * PIECE)
         multiply(1, 0, P)
         multiply(1, P, P)

@@ -251,9 +251,9 @@ def tile_list_heads_tm_hl_bias_kernel(tc, xT, w, wgt, b, offs, out):
                         stop=(a == PASSES - 1 and part == 1),
                     )
 
-        def finish(j, n0, n1):
-            nc.vector.tensor_tensor(out=result[j][:, n0:n1], in0=acc[j][:, n0:n1], in1=bias[:, n0:n1], op=ALU.add)
-            nc.sync.dma_start(out=out[j * P : (j + 1) * P, n0:n1], in_=result[j][:, n0:n1])
+        def finish(j):
+            nc.vector.tensor_tensor(out=result[j][:], in0=acc[j][:], in1=bias[:], op=ALU.add)
+            nc.sync.dma_start(out=out[j * P : (j + 1) * P, :], in_=result[j][:])
 
         half_rows = wgt.rearrange("p (h c) -> (p h) c", h=2)
         nc.sync.dma_start(out=wgt_rows[WGT_ROW0:P, :], in_=half_rows[0 : 2 * P : 2 * GROUPS + 1, :])
@@ -336,8 +336,5 @@ def tile_list_heads_tm_hl_bias_kernel(tc, xT, w, wgt, b, offs, out):
         round_all(1, S - P, P)
         for j0, c in ((PIECE, PIECE), (HALF_S, PIECE), (S - 2 * P, P), (S - P, P)):
             multiply(1, j0, c)
-        last = S // P - 1
-        for j in range(last):
-            finish(j, 0, M)
-        for n0 in (0, HALF_M):
-            finish(last, n0, n0 + HALF_M)
+        for j in range(S // P):
+            finish(j)

import concourse.mybir as mybir
from concourse.masks import make_identity

K, M, T, S = 1024, 512, 2048, 1024
P = 128
PACK = 4
PASSES = K // (P * PACK)
GROUPS = 8
PER_OFFSET_COLUMN = 16
RUN = 4

F32 = mybir.dt.float32
BF16 = mybir.dt.bfloat16
I32 = mybir.dt.int32
U32 = mybir.dt.uint32
U16 = mybir.dt.uint16
U8 = mybir.dt.uint8
FP8X4 = mybir.dt.float8_e4m3fn_x4
ALU = mybir.AluOpType
ACT = mybir.ActivationFunctionType

FLOPS = 2 * 2 * K * M * S
HI_MASK = -0x00100000
SIGN_BIT = -0x80000000

HALF_S = S // 2
HALF_M = M // 2
PART = M * PACK
WGT_ROW0 = P - 2 * GROUPS
PIECE = 2 * P
FIRST_LOADS = tuple((n0, n0 + P) for n0 in range(0, M, P))
PLANE_ORDER = tuple((a, i) for a in range(PASSES) for i in range(PACK))


def tile_list_heads_tm_hl_bias_kernel(tc, xT, w, wgt, b, offs, out):
    nc = tc.nc
    x_view = xT.rearrange("(a p i) t -> a i p t", a=PASSES, i=PACK)
    w_view = w.rearrange("(a p i) n -> a p i n", a=PASSES, i=PACK)

    with (
        tc.tile_pool(name="lists", bufs=1) as lists,
        tc.tile_pool(name="keep", bufs=1) as keep,
        tc.psum_pool(name="psum", bufs=1) as psum,
    ):
        offsets = lists.tile([P, S // PER_OFFSET_COLUMN], U16, name="offsets")
        wgt_sb = keep.tile([P, S], F32, name="wgt_sb", align_bytes=256)
        wgt_rows = keep.tile([P, HALF_S], F32, name="wgt_rows", align_bytes=256)
        room = keep.tile([P, 2 * PART], BF16, name="room", align_bytes=256)
        first_lo, first_hi = (
            room[:, part * PART : (part + 1) * PART].rearrange("p (n i) -> p n i", i=PACK) for part in range(2)
        )
        turned = room[:, PART : 2 * PART].bitcast(F32)
        bias = keep.tile([P, M], F32, name="bias", align_bytes=256)
        planes = [[keep.tile([P, T], F32, name=f"plane{a}{i}", align_bytes=256) for i in range(PACK)] for a in range(PASSES)]
        w_first = {n0: keep.tile([P, PACK, n1 - n0], F32, name=f"w_first{n0}", align_bytes=256) for n0, n1 in FIRST_LOADS}
        w_second = [keep.tile([P, PACK, HALF_M], F32, name=f"w_second{h}", align_bytes=256) for h in range(2)]
        ident = keep.tile([P, P], F32, name="ident", align_bytes=256)
        w_codes = [keep.tile([P, 2 * M], U32, name=f"w_codes{a}", align_bytes=256) for a in range(PASSES)]
        w_scales = [keep.tile([P, 2 * M], U8, name=f"w_scales{a}", align_bytes=256) for a in range(PASSES)]
        early_hi = keep.tile([P, HALF_S], F32, name="early_hi", align_bytes=256)
        lo_tiles = [keep.tile([P, HALF_S], F32, name=f"second_lo{h}", align_bytes=256) for h in range(2)]
        picked_flat = [keep.tile([P, PACK * S + PIECE], F32, name=f"picked{a}", align_bytes=256) for a in range(PASSES)]
        picked = [
            flat[:, at : at + PACK * S].rearrange("p (i j) -> p i j", i=PACK)
            for flat, at in zip(picked_flat, (PIECE, 0))
        ]

        def lodged(a, at):
            return picked_flat[a][:, at : at + HALF_S].bitcast(BF16)

        hi32 = picked_flat[1][:, 5 * PIECE : 13 * PIECE].rearrange("p (i n) -> p i n", i=PACK)
        neg_hi = picked_flat[1][:, 9 * PIECE : 13 * PIECE].rearrange("p (i n) -> p i n", i=PACK)
        second_hi = (early_hi[:].bitcast(BF16), lodged(0, 0))
        second_lo = [tile[:].bitcast(BF16) for tile in lo_tiles]
        early_words = lodged(1, 7 * PIECE)
        lo_words = (
            early_words[:, 0:HALF_S],
            early_words[:, HALF_S:S],
            lodged(0, PIECE + S)[:, 0:HALF_S],
            lodged(1, 15 * PIECE - P)[:, 0:HALF_S],
        )
        first_places = tuple(PIECE * at for at in (7, 8, 9, 10, 11, 13, 12, 14))
        x_first = lodged(1, PACK * S - PIECE)
        mask_columns = [flat[:, at : at + 1].bitcast(I32) for flat, at in ((picked_flat[0], PIECE + 2 * S), (picked_flat[1], 0))]
        x_second = lodged(0, 3 * S)
        x_late = keep.tile([P, HALF_S, PACK], BF16, name="x_late", align_bytes=256)
        x_codes = [keep.tile([P, S], U32, name=f"x_codes{a}", align_bytes=256) for a in range(PASSES)]
        x_scales = [keep.tile([P, S], U8, name=f"x_scales{a}", align_bytes=256) for a in range(PASSES)]
        acc = [psum.tile([P, M], F32, name=f"acc{j}") for j in range(S // P)]
        result = [keep.tile([P, M], F32, name=f"result{j}", align_bytes=256) for j in range(S // P)]

        def by_runs(tile_view, axes):
            return tile_view.rearrange(axes + " -> p c i e", e=RUN)

        def interleaved(tile_view):
            return by_runs(tile_view, "p (c e) i")

        def planar(tile_view):
            return by_runs(tile_view, "p i (c e)")


        def turn_wgt(v):
            bank = acc[2 + v]
            for u in range(2):
                at = (2 * v + u) * P
                nc.tensor.transpose(bank[:, u * P : (u + 1) * P], wgt_rows[:, at : at + P], ident[:])
            nc.scalar.copy(
                out=turned.rearrange("j (u h g r) -> j h u g r", h=2, u=4, g=GROUPS)[:, :, 2 * v : 2 * v + 2, :, :],
                in_=bank[:, 0 : 2 * P]
                .rearrange("j (u q) -> j u q", u=2)[:, :, WGT_ROW0:]
                .rearrange("j u (g h) -> j h u g", h=2)
                .unsqueeze(4)
                .to_broadcast([P, 2, 2, GROUPS, P // GROUPS]),
            )

        def spread_wgt(h):
            for block in range(HALF_S // P):
                at = (2 * block + h) * P
                nc.tensor.transpose(acc[h][:, block * P : (block + 1) * P], turned[:, at : at + P], ident[:])

        def fetch_wgt(h):
            nc.scalar.copy(out=wgt_sb[:, h * HALF_S : (h + 1) * HALF_S], in_=acc[h][:])


        def w_block(at, c):
            return w_first[at // P * P][:, :, at % P : at % P + c]

        def mask_first(at, c):
            nc.vector.tensor_scalar(
                out=hi32[:, :, at : at + c].bitcast(I32),
                in0=w_block(at, c).bitcast(I32),
                scalar1=HI_MASK,
                scalar2=None,
                op0=ALU.bitwise_and,
            )

        def subtract_first(at, c):
            nc.vector.tensor_tensor(
                out=interleaved(first_lo[:, at : at + c, :]),
                in0=planar(w_block(at, c)),
                in1=planar(hi32[:, :, at : at + c]),
                op=ALU.subtract,
            )

        def cast_first(at):
            nc.scalar.copy(out=interleaved(first_hi[:, at : at + P, :]), in_=planar(hi32[:, :, at : at + P]))


        def mask_second(h):
            nc.vector.tensor_scalar(
                out=neg_hi.bitcast(I32),
                in0=w_second[h][:].bitcast(I32),
                scalar1=mask_columns[h],
                scalar2=SIGN_BIT,
                op0=ALU.bitwise_and,
                op1=ALU.bitwise_xor,
            )

        def cast_second(h):
            target = second_hi[h].rearrange("p (n i) -> p n i", i=PACK)
            nc.scalar.activation(out=interleaved(target), in_=planar(neg_hi), func=ACT.Copy, scale=-1.0)

        def turn_lo(nb):
            bank = acc[(0, 1, 1, 0)[nb]]
            cols = slice(nb % 2 * P, (nb % 2 + 1) * P)
            for n, source in enumerate((w_second[nb // 2], neg_hi)):
                for i in range(PACK):
                    nc.tensor.matmul(
                        bank[:, i * P : (i + 1) * P],
                        lhsT=source[:, i, cols],
                        rhs=ident[:],
                        start=(n == 0 and i == 0),
                        stop=(n == 1 and i == PACK - 1),
                        is_transpose=True,
                    )
            nc.scalar.copy(
                out=lo_words[nb].rearrange("n (u p e) -> n u p e", u=2, e=2),
                in_=bank[:].rearrange("n (u e p) -> n u p e", u=2, e=2),
            )

        def turn_lo_back(h):
            bank = acc[h]
            for u in range(2):
                for block in range(2):
                    words = lo_words[2 * h + block].bitcast(F32)[:, u * P : (u + 1) * P]
                    to = (2 * u + block) * P
                    nc.tensor.transpose(bank[:, to : to + P], words, ident[:])
            nc.scalar.copy(
                out=second_lo[h].bitcast(F32).rearrange("p (n u) -> p n u", u=2),
                in_=bank[:].rearrange("p (u n) -> p n u", u=2),
            )

        def quantize_w(a, at, values):
            c = values.shape[1] // PACK
            nc.vector.quantize_mx(
                out=w_codes[a][:, at : at + c].bitcast(FP8X4),
                scales=w_scales[a][:, at : at + c],
                in_=values,
            )


        def gather(a, i, j0, c):
            nc.vector.tensor_tensor(
                out=picked[a][:, i, j0 : j0 + c],
                in0=planes[a][i][:].indirect(offsets[:, j0 // PER_OFFSET_COLUMN : (j0 + c) // PER_OFFSET_COLUMN]),
                in1=wgt_sb[:, j0 : j0 + c],
                op=ALU.mult,
            )

        def rounded(a, j0, c):
            if a == 1 and j0 >= HALF_S:
                return x_late[:, j0 - HALF_S : j0 - HALF_S + c, :]
            if a == 0:
                at = first_places[j0 // P]
                return picked_flat[1][:, at : at + 2 * c].bitcast(BF16).rearrange("p (j i) -> p j i", i=PACK)
            piece = (x_first, x_second)[j0 // PIECE]
            return piece.rearrange("p (j i) -> p j i", i=PACK)[:, j0 % PIECE : j0 % PIECE + c, :]

        def round_all(a, j0, c):
            nc.scalar.copy(out=interleaved(rounded(a, j0, c)), in_=planar(picked[a][:, :, j0 : j0 + c]))

        def round_first(j0):
            at, then = first_places[j0 // P : j0 // P + 2]
            both = picked_flat[1][:, at : 2 * then - at].bitcast(BF16).rearrange("p (b r) -> p b r", b=2)
            nc.scalar.copy(
                out=both[:, :, 0 : PACK * P].rearrange("p b (c e i) -> p b c i e", e=RUN, i=PACK),
                in_=picked[0][:, :, j0 : j0 + PIECE].rearrange("p i (b c e) -> p b c i e", b=2, e=RUN),
            )

        def round_pair(u, j0, c):
            pair = slice(2 * u, 2 * u + 2)
            nc.scalar.copy(out=interleaved(rounded(1, j0, c)[:, :, pair]), in_=planar(picked[1][:, pair, j0 : j0 + c]))

        def multiply(a, j0, c):
            nc.vector.quantize_mx(
                out=x_codes[a][:, j0 : j0 + c].bitcast(FP8X4),
                scales=x_scales[a][:, j0 : j0 + c],
                in_=rounded(a, j0, c).rearrange("p j i -> p (j i)"),
            )
            for j in range(j0 // P, (j0 + c) // P):
                cols = slice(j * P, (j + 1) * P)
                for part in range(2):
                    w_cols = slice(part * M, (part + 1) * M)
                    nc.tensor.matmul_mx(
                        out=acc[j][:],
                        lhsT=x_codes[a][:, cols].bitcast(FP8X4),
                        lhsT_scale=x_scales[a][:, cols],
                        rhs=w_codes[a][:, w_cols].bitcast(FP8X4),
                        rhs_scale=w_scales[a][:, w_cols],
                        start=(a == 0 and part == 0),
                        stop=(a == PASSES - 1 and part == 1),
                    )

        def finish(j):
            nc.vector.tensor_tensor(out=result[j][:], in0=acc[j][:], in1=bias[:], op=ALU.add)
            nc.sync.dma_start(out=out[j * P : (j + 1) * P, :], in_=result[j][:])

        half_rows = wgt.rearrange("p (h c) -> (p h) c", h=2)
        nc.sync.dma_start(out=wgt_rows[WGT_ROW0:P, :], in_=half_rows[0 : 2 * P : 2 * GROUPS + 1, :])
        for n0, n1 in FIRST_LOADS:
            nc.sync.dma_start(out=w_first[n0][:], in_=w_view[0][:, :, n0:n1])
        nc.sync.dma_start(offsets[:], offs)
        for n, (a, i) in enumerate(PLANE_ORDER):
            nc.sync.dma_start(out=planes[a][i][:], in_=x_view[a, i])
            if n in (1, 3):
                nc.sync.dma_start(out=w_second[n // 2][:], in_=w_view[1][:, :, n // 2 * HALF_M : (n // 2 + 1) * HALF_M])
        nc.sync.dma_start(out=bias[:], in_=b.partition_broadcast(P))

        nc.vector.memset(ident[:], 0.0)
        make_identity(nc, ident[:], nomemset=True)
        nc.vector.memset(wgt_rows[0:WGT_ROW0, :], 0.0)
        for v in range(2):
            turn_wgt(v)
        for h in range(2):
            spread_wgt(h)
        for column in mask_columns:
            nc.vector.memset(column, HI_MASK)
        for at, c in ((0, P // 2), (P, P // 2), (2 * P, P)):
            for step in (mask_first, subtract_first):
                step(at, c)
                step(at + c, c)
        quantize_w(0, 0, room[:, 0 : PART - PACK * P])
        quantize_w(0, M - P, room[:, PART - PACK * P : PART])
        for h in range(2):
            fetch_wgt(h)
        for at in range(0, M, P):
            cast_first(at)
        gather(0, 0, 0, HALF_S)
        gather(0, 0, HALF_S, HALF_S)
        gather(0, 1, 0, S)

        def split_second(h):
            cast_second(h)
            for nb in (2 * h, 2 * h + 1):
                turn_lo(nb)
            turn_lo_back(h)

        mask_second(0)
        quantize_w(0, M, room[:, PART : 2 * PART])
        split_second(0)
        gather(0, 2, 0, S)
        for j0 in (0, HALF_S):
            gather(0, 3, j0, HALF_S)
        mask_second(1)
        quantize_w(1, 0, second_hi[0])
        gather(1, 0, 0, S)
        quantize_w(1, M, second_lo[0])
        round_first(0)
        split_second(1)
        round_first(PIECE)
        round_first(HALF_S)
        round_first(S - PIECE)
        multiply(0, 0, P)
        multiply(0, P, P)
        gather(1, 1, 0, S)
        multiply(0, PIECE, PIECE)
        quantize_w(1, HALF_M, second_hi[1])
        multiply(0, 4 * P, P)
        multiply(0, 5 * P, P)
        gather(1, 2, 0, S)
        quantize_w(1, M + HALF_M, second_lo[1])
        multiply(0, 6 * P, P)
        multiply(0, 7 * P, P)

        gather(1, 3, 0, PIECE)
        round_pair(0, 0, PIECE)
        round_pair(0, PIECE, PIECE)
        round_pair(1, 0, PIECE)
        gather(1, 3, PIECE, S - 2 * PIECE)
        multiply(1, 0, P)
        multiply(1, P, P)
        gather(1, 3, S - PIECE, PIECE)
        round_pair(1, PIECE, PIECE)
        round_all(1, HALF_S, PIECE)
        round_all(1, S - 2 * P, P)
        round_all(1, S - P, P)
        for j0, c in ((PIECE, PIECE), (HALF_S, PIECE), (S - 2 * P, P), (S - P, P)):
            multiply(1, j0, c)
        for j in range(S // P):
            finish(j)
